import numpy as np, ml_dtypes
CORES = [25,29,65,69,153,157,193,197]
N = 8
BF = ml_dtypes.bfloat16
W, I, B, S, RO, H = 4096, 256, 16, 5, 3, 9
def some(rng, k):
    o = np.argsort(rng.random(k.shape[:-1] + (16,) + k.shape[-1:]), axis=-2)
    return np.where(o < k[..., None, :], 0, 255)
def parts(rng):
    x = rng.integers(0, 256, (N, 8, 16, W)); w = rng.integers(0, 16, (N, 8, 16, 1)); c = rng.integers(0, 128, (N, 8, 16, I))
    l = rng.integers(1, 5, (N, 8, 16, I)); s = rng.integers(0, W, (N, 8, 16, I))
    v = rng.choice(np.array([96, 176, 208, 224, 236, 244, 252]), (N, 8, 1, I))
    return x, w, c, l, s, np.clip(v + rng.integers(-12, 13, (N, 8, 16, I)), 0, 255)
def small(a):
    return np.ascontiguousarray(a.reshape(N, 128, -1)).astype(np.float32).astype(BF)
def pack(x, w, c, l, s, fl):
    return {"x": small(x), "wt": small(w), "ch": small(c), "sp": small(l), "st": np.ascontiguousarray(s.reshape(N, 128, I)).astype(np.int32), "fl": small(fl)}
def setup_inputs(rng):
    return pack(*parts(rng))
def setup_inputs_spread(rng):
    x, w, c, l, s, fl = parts(rng)
    x = (np.exp2(8 * rng.random((N, 8, 1, W))) * rng.random(x.shape)).astype(np.int64)
    w = np.where(rng.random(w.shape) < 0.4, 0, w)
    c = np.where(rng.random((N, 8, 1, I)) < 0.5, c, np.exp2(7 * rng.random(c.shape)).astype(np.int64) - 1)
    l = rng.choice(np.array([1, 1, 1, 2, 3, 4]), l.shape)
    fl = (np.exp2(8 * rng.random((N, 8, 1, I))) * (0.5 + 0.5 * rng.random(fl.shape))).astype(np.int64)
    return pack(x, w, c, l, s, fl)
def setup_inputs_ends(rng):
    x, w, c, l, s, fl = parts(rng)
    d = rng.choice(np.array([0.04, 0.1, 0.3, 0.5]), (N, 8, 1, 1)); d[:, 7] = 0.5
    e = 255 * (rng.random(x.shape) < d); k = rng.random((N, 8, 1, W)); full = np.where(np.arange(8) == 7, 0.3, 0.03).reshape(1, 8, 1, 1)
    e = np.where(k < full, 255, np.where(k > 0.85, 0, e)); x = np.where((k > 0.5) & (k < 0.6), x, e)
    w = 15 * rng.integers(0, 2, w.shape); w[:, 7] = 15; w[:, 1] = 0; w[:, 0, 0] = 0; w[:, 0, 15] = 15
    b = rng.random((N, 8, 1, I)); c = np.where(b < 0.15, 127, np.where(b > 0.85, 0, 127 * rng.integers(0, 2, c.shape)))
    l = 1 + 3 * rng.integers(0, 2, l.shape); s = np.where(rng.random(s.shape) < 0.25, s, (W - 1) * rng.integers(0, 2, s.shape))
    fl = some(rng, rng.integers(0, 17, (N, 8, I))); fl[N - 2:] = some(rng, rng.integers(H, 17, (2, 8, I)))
    x[N - 2, 6, H - 1:] = 0; fl[N - 2, 6, :, I - 1] = np.where(np.arange(16) < H - 1, 0, 255)
    l[N - 1, 7, :, :2] = 4; s[N - 1, 7, :, :2] = W - 1
    l[N - 1, 7, 13:, I - 1] = np.array([1, 4, 4]); s[N - 1, 7, 13:, I - 1] = np.array([(0 - 613) & (W - 1), (W - 1 - 2452) & (W - 1), W - 1])
    c[N - 1, 7, 0, :2] = 127; c[N - 1, 7, 0, I - 1] = 127
    x[:, 7, :, (W - 1 + 2452) & (W - 1)] = 255; x[:, 7, :, W - 1] = 255; x[:, 7, 15] = 255
    return pack(x, w, c, l, s, fl)
def setup_inputs_corners(rng):
    x, w, c, l, s, fl = parts(rng); q = rng.permutation(N); ar = np.arange(16)[:, None]
    w[:, 0] = 0; b = rng.integers(0, 4, (N, 1, I)); c[:, 0] = np.where(b == 0, 3, np.where(b == 1, 0, np.where(b == 2, 127, c[:, 0])))
    x[:, 1] = np.minimum(x[:, 1], 254); fl[:, 1] = some(rng, rng.choice(np.array([0, H - 1, H, 16]), (N, I)))
    v = rng.integers(1, 255, (N, 16, 1)); x[:, 2] = v; fl[:, 2] = v + np.minimum(some(rng, rng.choice(np.array([H - 1, H, 16]), (N, I))), 1)
    w[:, 3] = 0; w[:, 3, 0] = 1; x[:, 3, 0, ::2] = 255; fl[:, 3] = fl[:, 3] // 2
    b = rng.integers(0, 4, (N, 1, I)); l[:, 4] = np.where(b == 0, 4, np.where(b == 1, 1, np.where(b == 2, 1 + 3 * (ar == 15), 1 + 3 * (ar & 1)))); fl[:, 4] = fl[:, 4] // 2
    e = (W - 1) * rng.integers(0, 2, (N, 16, I)); s[:, 5] = np.where(rng.random((N, 16, I)) < 0.5, e, (e - 613 * l[:, 5]) & (W - 1))
    w[:, 6] = 15; x[:, 6] = rng.integers(224, 256, (N, 16, W)); c[:, 6] = rng.choice(np.array([0, 126, 127]), (N, 16, I))
    x[q[0]] = np.minimum(x[q[0]], 254); fl[q[0]] = some(rng, np.full((8, I), H - 1))
    fl[q[1]] = some(rng, rng.integers(H, 17, (8, I))); fl[q[2]] = some(rng, rng.integers(H, 17, (8, I)))
    x[q[2], 7] = np.minimum(x[q[2], 7], 254); fl[q[2], 7, :, I - 1] = some(rng, np.full(1, H - 1))[:, 0]
    return pack(x, w, c, l, s, fl)
def setup_inputs_crowd(rng):
    x, w, c, l, s, fl = parts(rng); q = rng.permutation(N)
    s[:, :7] = rng.integers(0, W, (N, 7, 1, 1)); l[:, :7] = rng.integers(1, 5, (N, 7, 1, 1)); c[:, :7] = rng.integers(0, 128, (N, 7, 16, 1))
    s[:, 4:7, 15, I - 1] = rng.integers(0, W, (N, 3)); c[:, 4:7, :, I - 1] = rng.integers(0, 128, (N, 3, 16))
    fl = some(rng, rng.integers(H, 17, (N, 8, I)))
    for a in q[:N // 2]:
        x[a, 7] = np.minimum(x[a, 7], 254); fl[a, 7, :, I - 1] = some(rng, np.full(1, H - 1))[:, 0]
    return pack(x, w, c, l, s, fl)
def setup_inputs_late(rng):
    x, w, c, l, s, fl = parts(rng); q = rng.permutation(N); a, b = int(q[0]), int(q[1])
    x[a] = np.minimum(x[a], 254); fl[a] = some(rng, np.full((8, I), H - 1)); fl[b] = some(rng, rng.integers(H, 17, (8, I)))
    for r, g, low in ((a, 7, 8), (b, 0, 0)):
        hot = B * int(rng.integers(8, I)); w[r, g] = 0
        x[r, g] = rng.integers(0, 101, (16, W)); x[r, g, :, hot] = rng.integers(200, 255, 16)
        fl[r, g, :, low:] = rng.integers(110, 151, (16, I - low))
        l[r, g] = 1; s[r, g] = (hot - 613) & (W - 1)
        if g == 7: l[(a - 2) % N, 7] = 1; s[(a - 2) % N, 7] = (hot - 613) & (W - 1)
    s[(a - 1) % N, 7] = (16 * rng.integers(0, W // 16, (16, I)) - (I - 8)) & (W - 1)
    l[(b - 1) % N, 0] = 1; s[(b - 1) % N, 0] = W - 613 - 8 * I
    c[(b - 1) % N, 0] = 16 * rng.integers(0, 8, (16, I)) + 4 * rng.integers(1, 4, (16, I))
    return pack(x, w, c, l, s, fl)
def check_inputs(d):
    bad = []
    for k, lo, hi in (("x", 0, 255), ("wt", 0, 15), ("ch", 0, 127), ("sp", 1, 4), ("st", 0, W - 1), ("fl", 0, 255)):
        v = np.asarray(d[k]).astype(np.float64)
        if not (np.all(v >= lo) and np.all(v <= hi)): bad.append("range of " + k)
        if np.any(v != np.floor(v)): bad.append("whole numbers of " + k)
    return bad
def reference(x, wt, ch, sp, st, fl):
    X, Q, C, L, Z, F = [v.astype(np.float32).astype(np.int32).reshape(N, 8, 16, -1) for v in (x, wt, ch, sp, st, fl)]
    A = [0] * N; row = np.arange(16)[:, None]
    for t in range(RO):
        if t > 0: C, L, Z = np.roll(C, 1, axis=0), np.roll(L, 1, axis=0), np.roll(Z, 1, axis=0)
        for a in range(N):
            l = L[a]
            at = np.arange(16)[None, :, None, None]; at = at + np.where(at >= row[None, None], l[:, None], 0)
            e = np.take_along_axis(np.concatenate([C[a], np.zeros((8, 4, I), np.int32)], axis=1)[:, :, None, :], at, 1)
            e = np.concatenate([e, np.zeros((8, 1, 16, I), np.int32)], axis=1)
            s = (Z[a] + 613 * l + A[a]) & (W - 1); p = np.zeros((8, 16, I), np.int64); V = np.zeros((8, 16, 16, I), np.int32); log = []
            for k in range(S):
                z = np.take_along_axis(X[a], s.reshape(8, 1, 16 * I), 2).reshape(8, 16, 16, I)
                V = np.maximum(V, z); c = np.take_along_axis(e, np.minimum(p, 16)[:, None], 1)[:, 0].astype(np.int64)
                u = np.add.reduce(Q[a][..., None] * z, axis=1).astype(np.int64)
                n = 1 + (((u >> 3) + c) & 3); log.append((p, n))
                s = (((u * (2 * c + 1)) >> 3) + 37 * u + c) & (W - 1); p = p + n
            fails = np.add.reduce((V >= F[a][:, :, None, :]).astype(np.int32), axis=1) >= H
            best = np.argmax(np.where(fails, 16 * l + 15 - row[None], 0 - 1), axis=1)[:, None, :]; ok = np.any(fails, axis=1)[:, None, :]
            nl = np.ones((8, 16, I), np.int64)
            for p, n in log: nl = np.where(row[None] == np.take_along_axis(p, best, 1), np.take_along_axis(n, best, 1), nl)
            v = np.take_along_axis(V, best[:, None], 2)[:, :, 0]
            C[a] = np.where(ok, np.take_along_axis(e[:, :16], best[:, None], 2)[:, :, 0], C[a]); L[a] = np.where(ok, nl, l)
            to = B * np.arange(I)[None, None, :] + (np.add.reduce(Q[a] * v, axis=1)[:, None, :] & (B - 1))
            to = np.broadcast_to(to, (8, 16, I)); np.put_along_axis(X[a], to, np.where(ok, v, np.take_along_axis(X[a], to, 2)), 2)
            F[a] = np.where(ok, (F[a] + v) >> 1, F[a]); A[a] = int(np.sum(ok))
    sums = np.add.reduce(X.reshape(N, 128, I, B), axis=3)
    return {"yc": C.reshape(N, 128, I).astype(np.float32).astype(BF), "yl": L.reshape(N, 128, I).astype(np.float32).astype(BF),
            "yf": F.reshape(N, 128, I).astype(np.float32).astype(BF), "ys": sums.astype(np.float32)}

@@ -1,0 +1,530 @@
+from concourse.mybir import AluOpType as OP, AxisListType, ActivationFunctionType as AF
+
+SLOTS = ["I", "B1", "ON", "LT", "LE", "S1", "S2", "S3", "S4", "E0", "E1", "E2", "E3", "I32", "I512", "I101", "I64", "mI",
+         "I16", "mB1", "mI4", "mB8", "BD32", "B512", "BX32", "BW", "BQ0", "T0", "T1", "T2", "T3", "DG0", "DG3"]
+SLOTS += ["L%d" % e for e in range(15)]
+SLOT = {n: j for j, n in enumerate(SLOTS)}
+BUF = {"bfloat16": "xt_8192 zz_20480 vs_20480 mk5_5120 wl_2064 cl_2064 mo_2064 ff_256 wtb_16 onef_16 e16_16 tmpm_128 k107_128 km1_128 kmh_128 kd_128 junk_128",
+       "float32": "sd_16 jio_16 jt_16 co_24 b8f_8 c80_8 c16_16 ac_16 ysb_256", "int32": "sti_256 tmi_256 tmj_256"}
+BUFH = {"bfloat16": "h0_512 h1_2048 h2_2048 h3_2048 t0_512 dt_2048 sc_2048 rd_640 hn_640 scn_640 gg_1024 c5_128 pt_512 pp_128 "
+                    "msk_128 tq_128 w3_128 fl_128 fw_128 cand_128 win_128 vsel_128 z4_128 wx_640 ax_384 ex_512 m4_128 t4_128 n4m_128",
+        "float32": "nk_8 f1_128", "int32": "s32_128 x32_128 r32_128 n32_128 nn_128 n4_128 n5_128 o32_8 q32_8", "uint16": "offs_128 ofs_8 of2_8"}
+
+
+def _bufs():
+    out = {"mats": ("sbuf", [128, len(SLOTS) * 128], "bfloat16")}
+    for table, hs in ((BUF, ("",)), (BUFH, ("a", "b"))):
+        for dt, names in table.items():
+            for s in names.split():
+                nm, n = s.split("_")
+                for h in hs:
+                    out[nm + h] = ("sbuf", [128, int(n)], dt)
+    for t in range(3):
+        out["rec%d" % t] = ("sbuf", [128, 1024], "bfloat16")
+        out["nr%d" % t] = ("sbuf", [128, 512], "bfloat16")
+    for h in "ab":
+        out["pu" + h] = out["pm" + h] = ("psum", [128, 512], "float32")
+        out["pd" + h] = ("psum", [128, 1024], "float32")
+    return out
+
+
+SCRATCH = _bufs()
+MSG = [("st", 1), ("st", 2)] + [(k + h, t) for t in (1, 2) for h in "ab" for k in "cl"]
+COLS = {"st": (512, 1024), "ca": (0, 128), "cb": (128, 256), "la": (256, 384), "lb": (384, 512)}
+SEMAPHORES = ["e_v", "e_s", "e_t", "e_g"] + ["ld_" + n for n in ("st", "sp", "wt", "x", "ch", "fl")] + ["o_c", "o_l", "o_f", "o_s"]
+SEMAPHORES += [p + "%s%d" % m for m in MSG for p in ("a_", "b_")]
+KEEP = []
+
+
+def nbits(m):
+    return bin(m).count("1")
+
+
+def relays(src, dst, topo):
+    if topo.may_write(src, dst):
+        return []
+    own = [c for c in topo.cores_of(src) if c != src and topo.may_write(c, dst)]
+    return sorted(own, key=lambda c: (topo.die(c) != topo.die(src), c))
+
+
+def via(msg, src, dst, topo):
+    own = relays(src, dst, topo)
+    return own[(msg[0][-1] == "a") % len(own)] if own else None
+
+
+def cv(n, k):
+    return 55 + max(64, n * k) * 0.95
+
+
+def cs(n, k=1):
+    return 65 + n * k * 0.95
+
+
+def order(nodes):
+    n = len(nodes)
+    pred, succ, lw, rd = [[] for _ in range(n)], [[] for _ in range(n)], {}, {}
+    for j, (alts, r, w, _) in enumerate(nodes):
+        ws = w + [t for t in r if t[0] == "#"]
+        ps = set()
+        for t in r + ws:
+            ps.update(lw.get(t, []) if t[0] != "+" else rd.get(t[1:], []))
+        for t in ws:
+            ps.update(rd.get(t, []))
+        for t in r:
+            rd.setdefault(t, []).append(j)
+        for t in ws:
+            if t[0] == "+":
+                lw.setdefault(t[1:], []).append(j)
+            else:
+                lw[t], rd[t] = [j], []
+        pred[j] = sorted(ps - {j})
+        for p in pred[j]:
+            succ[p].append(j)
+    prio = [0.0] * n
+    for j in range(n - 1, -1, -1):
+        prio[j] = nodes[j][0][0][1] + 80 + max([prio[x] for x in succ[j]] + [0])
+    for j in range(n):
+        if any(t[-1] == "a" for t in nodes[j][2]):
+            prio[j] += 3000
+    left = [len(p) for p in pred]
+    ready = [j for j in range(n) if not left[j]]
+    free, end, qof, out = {}, [0.0] * n, [None] * n, []
+    while ready:
+        c = []
+        for j in ready:
+            best = None
+            for a, alt in enumerate(nodes[j][0]):
+                q, cost = alt[0], alt[1]
+                s = free.get(q, 0.0) if q != "n" else 0.0
+                for p in pred[j]:
+                    s = max(s, end[p] + (20 if qof[p] == q else 80))
+                if best is None or s + cost < best[0]:
+                    best = (s + cost, s, a, q)
+            c.append((best, j))
+        e, j = min(c, key=lambda x: (x[0][1], -prio[x[1]]))
+        t0, q0 = e[1], e[3]
+        e, j = max([x for x in c if x[0][3] == q0 and x[0][1] <= t0 + 100], key=lambda x: (prio[x[1]], -x[1]))
+        fin, s, a, q = e
+        ready.remove(j)
+        end[j], qof[j] = fin, q
+        free[q] = s + 70 if nodes[j][3] == "dma" else fin
+        out.append((s, j, a))
+        for x in succ[j]:
+            left[x] -= 1
+            if not left[x]:
+                ready.append(x)
+    return out
+
+
+def rank_program(g, core, T, topo):
+    N = len(T.cores)
+    rank = T.rank_of(core)
+
+    def put(msg, src_ap, dst):
+        a, b = COLS[msg[0]]
+        rid, pid = topo.addr(dst, core)
+        m = topo.mask(core, dst)
+        g.remote_dma(T["rec%d" % msg[1]][:, a:b], src_ap, T.sem["a_%s%d" % msg], T.sem["b_%s%d" % msg], pid, rid, m)
+        return nbits(m)
+
+    if rank is None:
+        for r in range(N):
+            src, dst = T.cores[r], T.cores[(r + 1) % N]
+            sent = []
+            for msg in [x for x in MSG if via(x, src, dst, topo) == core]:
+                a, b = COLS[msg[0]]
+                g.wait_ge(T.sem["a_%s%d" % msg], nbits(topo.mask(src, core)))
+                sent.append((msg, put(msg, T["rec%d" % msg[1]][:, a:b], dst)))
+            for msg, n in sent:
+                g.wait_ge(T.sem["b_%s%d" % msg], n)
+        return
+
+    nxt, prv = T.cores[(rank + 1) % N], T.cores[(rank - 1) % N]
+    nodes = []
+
+    def add(alts, r, w, kind="op"):
+        nodes.append((alts, list(r), list(w), kind))
+
+    def vop(meth, cost, r, w, *a):
+        add([("v", cost, lambda: {"tt": g.vector.tensor_tensor, "ts": g.vector.tensor_scalar, "tc": g.vector.tensor_copy, "ms": g.vector.memset,
+                                  "sc": g.vector.tensor_tensor_scan, "tr": g.vector.tensor_reduce}[meth](*a))], r, w)
+
+    def tt(out, a, b, op, r, w, c=128):
+        vop("tt", cv(c, 1), r, w, out, a, b, op)
+
+    def ts(out, a, s1, s2, o1, o2, r, w, c=64):
+        vop("ts", cv(c, 1), r, w, *((out, a, s1, s2, o1) if o2 is None else (out, a, s1, s2, o1, o2)))
+
+    def tc(out, a, r, w, c=128):
+        vop("tc", cv(c, 1), r, w, out, a)
+
+    def ms(ap, val, w, c=64):
+        vop("ms", cv(c, 1), [], w, ap, val)
+
+    def scan(out, a, b, o1, r, w, n):
+        vop("sc", cv(n, 0.5), r, w, out, a, b, 0.0, OP.mult, o1)
+
+    def act(out, in_, func, r, w, n=128, k=1, **kw):
+        add([("s", cs(n, k), lambda: g.scalar.activation(out, in_, func, **kw))], r, w)
+
+    def gp(meth, r, w, *a, **kw):
+        add([("g", 350, lambda: {"iota": g.iota, "sel": g.affine_select}[meth](*a, **kw))], r, w)
+
+    def MM(r, w, items, ns):
+        def f():
+            for o, l, x, s0, s1 in items:
+                i = g.tensor.matmul(o, l, x, s0, s1)
+            return i
+        add([("t", 60 + 0.45 * max(64, ns) * len(items), f)], r, w)
+
+    def grp(out, pairs):
+        return [(out, l, x, j == 0, j == len(pairs) - 1) for j, (l, x) in enumerate(pairs)]
+
+    def M(n):
+        return T.mats[:, SLOT[n] * 128:SLOT[n] * 128 + 128]
+
+    def WM(n, m):
+        return T[n][:, 128 * m:128 * m + 128]
+
+    def dma(q, sem, out, in_, r, w, cost=2600):
+        add([(q, cost, lambda: {"y": g.sync, "s": g.scalar}[q].dma_start(out, in_))], r, w, ("dma", sem, 16))
+
+    dma("s", "ld_st", T.sti[:], T.st[:], [], ["sti"])
+    dma("s", "ld_sp", T.rec0[:, 256:512], T.sp[:], [], ["l0a", "l0b"])
+    dma("s", "ld_wt", T.wtb[:, 0:1], T.wt[:], [], ["wtb"])
+    dma("y", "ld_x", T.xt[:, 0:4096], T.x[:], [], ["x"], 8000)
+    dma("s", "ld_ch", T.rec0[:, 0:256], T.ch[:], [], ["c0a", "c0b"])
+    dma("s", "ld_fl", T.ff[:], T.fl[:], [], ["ffa", "ffb"])
+    ms(M("ON"), 1.0, ["ON"]); ms(T.onef[:], 1.0, ["onef"])
+    for nm in ("wl", "cl", "mo"):
+        ms(T[nm][:], 0.0, [nm + "0"], 1032)
+    for nm, st in (("jio", [[1, 16]]), ("c80", [[1280, 8]]), ("c16", [[256, 16]])):
+        gp("iota", [], [nm], T[nm][:], st, 0, 0, allow_small_or_imprecise_dtypes=True)
+    gp("sel", ["ON"], ["I"], M("I"), M("ON"), [[-1, 128]], OP.is_equal, 0.0, 0, 1)
+    gp("sel", ["ON"], ["tmpm"], T.tmpm[:], M("ON"), [[-16, 8], [0, 16]], OP.is_ge, 0.0, 0, 1)
+    gp("sel", ["tmpm"], ["B1"], M("B1"), T.tmpm[:], [[16, 8], [0, 16]], OP.is_ge, 0.0, 15, -1)
+    gp("sel", ["B1"], ["LT"], M("LT"), M("B1"), [[1, 128]], OP.is_gt, 0.0, 0, -1)
+    gp("sel", ["B1"], ["LE"], M("LE"), M("B1"), [[1, 128]], OP.is_ge, 0.0, 0, -1)
+    for d in (1, 2, 3, 4):
+        gp("sel", ["B1"], ["S%d" % d], M("S%d" % d), M("B1"), [[-1, 128]], OP.is_equal, 0.0, -d, 1)
+    ts(T.tmi[:], T.sti[:], 6, None, OP.arith_shift_right, None, ["sti"], ["tmi"], 256)
+    ts(T.tmj[:], T.sti[:], 63, None, OP.bitwise_and, None, ["sti"], ["tmj"], 256)
+    tc(T.rec0[:, 512:768], T.tmi[:], ["tmi"], ["+s0"], 256)
+    tc(T.rec0[:, 768:1024], T.tmj[:], ["tmj"], ["+s0"], 256)
+    tt(T.junk[:, 0:64], T.mats[:, 0:64], T.mats[:, 64:128], OP.add, ["I"], ["f64"])
+    tt(T.junk[:, 64:96], T.junk[:, 0:32], T.junk[:, 32:64], OP.add, ["f64"], ["f32"])
+    tt(T.e16[:], T.junk[:, 64:80], T.junk[:, 80:96], OP.add, ["f32"], ["e16"])
+    tt(T.jt[:], T.e16[:], T.jio[:], OP.mult, ["e16", "jio"], ["jt"])
+    co = lambda j: T.co[:, j:j + 1]
+    vop("tr", 120, ["jt"], ["co0"], co(0), T.jt[:], AxisListType.X, OP.add)
+    for k in (1, 2, 3):
+        ts(co(k), co(0), float(-k), None, OP.add, None, ["co0"], ["co%d" % k])
+        ts(co(4 + k), co(0), -1.0, float(k), OP.mult, OP.add, ["co0"], ["co%d" % (4 + k)])
+    ts(co(4), co(0), 28.0, None, OP.add, None, ["co0"], ["co4"])
+    ts(co(8), co(0), 5.0, 4.0, OP.mult, OP.add, ["co0"], ["co8"])
+    ts(co(9), T.wtb[:, 0:1], 64.0, None, OP.mult, None, ["wtb"], ["co9"])
+    ts(co(10), co(0), 80.0, None, OP.mult, None, ["co0"], ["co10"])
+    ts(co(11), co(0), 16.0, None, OP.mult, None, ["co0"], ["co11"])
+    ts(co(12), T.e16[:, 0:1], 1.0, None, OP.mult, None, ["e16"], ["co12"])
+    ts(co(13), T.e16[:, 0:1], -1.0, 1.0, OP.mult, OP.add, ["e16"], ["co13"])
+    ts(T.c80[:], T.c80[:], co(10), None, OP.add, None, ["co10", "c80"], ["c80"])
+    ts(T.c16[:], T.c16[:], co(11), None, OP.add, None, ["co11", "c16"], ["c16"])
+    b8 = SLOT["B1"] * 128
+    tc(T.b8f[:], T.mats[:, b8:b8 + 113:16], ["B1"], ["b8f"])
+    for gi in range(8):
+        colb = T.b8f[:, gi:gi + 1]
+        sl = slice(16 * gi, 16 * gi + 129 * 15 + 1, 129)
+        ts(T.wl[:, sl], T.onef[:], co(9), colb, OP.mult, OP.mult, ["onef", "co9", "b8f", "wl0"], ["+wl"])
+        ts(T.cl[:, sl], T.onef[:], colb, None, OP.mult, None, ["onef", "b8f", "cl0"], ["+cl"])
+        ts(T.mo[:, sl], T.onef[:], co(8), colb, OP.mult, OP.mult, ["onef", "co8", "b8f", "mo0"], ["+mo"])
+    tt(T.sd[:, 1:15], T.e16[:, 1:15], T.e16[:, 2:16], OP.subtract, ["e16"], ["+sd"])
+    tc(T.sd[:, 15:16], T.e16[:, 15:16], ["e16"], ["+sd"])
+    tc(T.sd[:, 0:1], T.e16[:, 0:1], ["e16"], ["+sd"])
+
+    def mat(dst, src, f, f2=None, r2=()):
+        ts(M(dst), M(src), f, f2, OP.mult, None if f2 is None else OP.mult, [src] + list(r2), [dst])
+
+    for nm, f in (("I512", 512.0), ("I101", 101.0), ("I64", 64.0), ("I32", 32.0), ("mI", -1.0), ("I16", 16.0), ("mI4", -4.0)):
+        mat(nm, "I", f)
+    mat("T0", "B1", T.sd[:, 0:1], 0.03125, ["sd"])
+    for e in range(4):
+        nm = "T%d" % e
+        if e:
+            ms(M(nm), 0.0, [nm])
+        o = SLOT[nm] * 128
+        sc = T.sd[:, e + 1:e + 2] if e < 3 else T.e16[:, 4:5]
+        ts(T.mats[:, o:o + 113:16], T.mats[:, b8:b8 + 113:16], sc, 0.03125, OP.mult, OP.mult, ["B1", "sd", "e16"], [nm])
+    mat("DG0", "I", co(13), None, ["co13"]); mat("DG3", "I", co(12), None, ["co12"])
+    for nm, v in (("kd", -215.0 / 64), ("k107", 107.5), ("km1", -1.0), ("kmh", -0.5)):
+        ms(T[nm][:], v, [nm])
+    for e in range(15):
+        mat("L%d" % e, "B1", T.sd[:, e + 1:e + 2], 0.03125, ["sd"])
+    for nm, f in (("mB1", -1.0), ("mB8", -8.0), ("BD32", 0.03125), ("B512", 512.0), ("BX32", 32.0)):
+        mat(nm, "B1", f)
+    mat("BW", "B1", co(9), None, ["co9"])
+    for d in range(4):
+        s0 = "S%d" % d if d else "I"
+        tt(M("E%d" % d), M(s0), M("S%d" % (d + 1)), OP.subtract, [s0, "S%d" % (d + 1)], ["E%d" % d], 256)
+    ms(M("BQ0"), 0.0, ["BQ0"])
+    o = SLOT["BQ0"] * 128
+    tc(T.mats[:, o:o + 113:16], T.mats[:, b8:b8 + 113:16], ["B1"], ["BQ0"])
+    ms(T.mk5[:], 1.0, ["mk5"], 2560)
+    ms(T.mk5[:, 0:5120:5], 0.0, ["mk5"], 1024)
+    ms(T.ac[:, 0:1], 0.0, ["ac0"])
+    for h in "ab":
+        ms(T["h0" + h][:], 0.0, ["h0z" + h], 256); ms(T["hn" + h][:], 0.0, ["hnz" + h], 320)
+        for k in (1, 2, 3):
+            nm = "h%d%s" % (k, h)
+            if k < 3:
+                ms(T[nm][:], 1.0, [nm], 1024)
+            for e in range(k):
+                ms(T[nm][:, e:2048:16], 0.0, [nm])
+
+    sends = []
+
+    def send(msg, ap, tags):
+        def f():
+            sends.append(("b_%s%d" % msg, put(msg, ap, via(msg, core, nxt, topo) or nxt)))
+        add([("g", 1500, f)], tags, ["sent%s%d" % msg], ("send",))
+        tag = {"st": "s%d", "ca": "c%da", "cb": "c%db", "la": "l%da", "lb": "l%db"}[msg[0]] % msg[1]
+        add([("n", 3500, None)], ["sent%s%d" % msg], [tag], ("arr", "a_%s%d" % msg, nbits(topo.mask(via(msg, prv, core, topo) or prv, core))))
+
+    send(("st", 1), T.rec0[:, 512:1024], ["s0"])
+
+    def places(t, h):
+        R, b, pm = T["rec%d" % t], 128 * (h == "b"), T["pm" + h]
+        L = R[:, 256 + b:384 + b]
+        MM(["I512", "I101", "I64", "I", "l%d" % t + h, "s%d" % t], ["#pm" + h],
+           grp(pm[:, 384:512], [(M("I512"), L), (M("I101"), L), (M("I64"), R[:, 512 + b:640 + b]), (M("I"), R[:, 768 + b:896 + b])]), 128)
+        ts(T["s32" + h][:], pm[:, 384:512], T.ac[:, 4 * t:4 * t + 1], None, OP.add, None, ["#pm" + h, "ac%d" % t], ["s32" + h], 128)
+        ts(T["r32" + h][:], T["s32" + h][:], 4095, None, OP.bitwise_and, None, ["s32" + h], ["r32" + h], 128)
+        tc(T["offs" + h][:], T["r32" + h][:], ["r32" + h], ["off" + h])
+
+    def gather(k, h):
+        for s in (0, 1):
+            c0 = 128 * (h == "b") + 64 * s
+            act(T.zz[:, 80 * c0 + k:80 * (c0 + 64) - 4 + k:5], T.xt[:, 0:4096].indirect(T["offs" + h][:, 64 * s:64 * s + 64]), AF.Copy,
+                ["x", "off" + h], ["z%d%s%d" % (k, h, s)], 1024, 1.5)
+
+    def stream(t, h):
+        b = 128 * (h == "b")
+        R = T["rec%d" % t]
+        C, L = R[:, b:b + 128], R[:, 256 + b:384 + b]
+        cg, lg = "c%d" % t + h, "l%d" % t + h
+        X = lambda nm: T[nm + h]
+        pu, pm, pd = X("pu"), X("pm"), X("pd")
+        PU, PM, D0, D1 = "#pu" + h, "#pm" + h, "#pd0" + h, "#pd1" + h
+        g_ = lambda *n: [x + h for x in n]
+        win, wx = X("win"), X("wx")
+
+        for e in range(4):
+            MM(["T%d" % e, "DG0", "DG3", "kd", cg], [D0],
+               grp(pd[:, e:509 + e:4], [(M("T%d" % e), C)] + ([(M("DG%d" % e), T.kd[:])] if e in (0, 3) else [])), 128)
+        act(X("t0")[:], pd[:, 0:512], AF.Copy, [D0], g_("t0"), 512)
+        ts(X("pp")[:], L, -1.0, co(12), OP.add, OP.mult, [lg, "co12"], g_("pp"))
+        for e in (1, 2, 3):
+            ts(X("h0")[:, e:512:4], X("pp")[:], float(e), None, OP.is_lt, None, g_("pp", "h0z"), ["+h0" + h])
+        scan(X("sc")[:, 0:512], X("h0")[:], X("t0")[:], OP.add, g_("h0", "t0"), g_("sc"), 512)
+
+        def c512(y, ys):
+            o, i = X("c5")[:], X("sc")[:, y:y + 127 * ys + 1:ys]
+            add([("s", cs(128), lambda: g.scalar.activation(o, i, AF.Identity, scale=16384.0, bias=55040.0)),
+                 ("v", cv(64, 1), lambda: g.vector.tensor_scalar(o, i, 16384.0, 55040.0, OP.mult, OP.add))], g_("sc"), g_("c5"))
+            return i
+
+        mv = c512(3, 4)
+        MM(["I", lg], [PM], grp(pm[:, 256:384], [(M("I"), L)]), 128)
+        for n in (0, 1):
+            it = []
+            for hb in (0, 1):
+                r0 = b + 64 * n + 32 * hb
+                for e in range(16):
+                    it += grp(pd[:, 512 * hb + e:512 * hb + e + 497:16], [(M("L%d" % e), R[:, r0:r0 + 32]) if e < 15 else (M("I"), T.kd[:, 0:32])])
+            MM(["L%d" % e for e in range(15)] + ["I", "kd", cg], [D0, D1], it, 32)
+            for hb in (0, 1):
+                c0 = 1024 * n + 512 * hb
+                act(X("dt")[:, c0:c0 + 512], pd[:, 512 * hb:512 * hb + 512], AF.Copy, [D1 if hb else D0], ["dt%d%s" % (2 * n + hb, h)], 512)
+        MM(["E0", "E1", "E2", "E3", "S4", cg], [D0, D1], [x for d in range(5) for x in grp(pd[:, 128 * d:128 * d + 128], [(M("E%d" % d if d < 4 else "S4"), C)])], 128)
+        for d in range(5):
+            act(X("rd")[:, d:640:5], pd[:, 128 * d:128 * d + 128], AF.Copy, [D1 if d == 4 else D0], ["rd%d%s" % (d, h)])
+        act(X("w3")[:], L, AF.Sigmoid, [lg], g_("w3"), scale=3.4657359027997265, bias=-41.58883083359672)
+
+        zb = 80 * b
+        for k in range(4):
+            kk = k + 1
+            gather(k, h)
+            U, U2 = pu[:, 0:128], pd[:, 0:128]
+            zt = ["wl", "z%d%s0" % (k, h), "z%d%s1" % (k, h)]
+            us = [(WM("wl", m), T.zz[:, zb + 5 * m + k:zb + 5 * m + k + 80 * 127 + 1:80]) for m in range(16)]
+            MM(zt, [PU], grp(U, us), 128)
+            tt(X("x32")[:], U, mv, OP.mult, [PU] + g_("sc"), g_("x32"))
+            tt(X("n32")[:], U, X("c5")[:], OP.add, [PU] + g_("c5"), g_("n32"))
+            MM(["I32", "I", "k107"] + zt + g_("sc"), [D0], grp(U2, [(M("I32"), mv), (M("I"), T.k107[:])] + us), 128)
+            ts(X("s32")[:], X("x32")[:], 3, 4095, OP.arith_shift_right, OP.bitwise_and, g_("x32"), g_("s32"), 128)
+            tt(X("r32")[:], X("s32")[:], U2, OP.add, [D0] + g_("s32"), g_("r32"))
+            ts(X("s32")[:], X("r32")[:], 4095, None, OP.bitwise_and, None, g_("r32"), g_("s32"), 128)
+            tc(X("offs")[:], X("s32")[:], g_("s32"), ["off" + h])
+            P = X("pt")[:, 128 * k:128 * kk]
+            tp = "p%d%s" % (kk, h)
+            ts(X("nn")[:], X("n32")[:], 9, 3, OP.arith_shift_right, OP.bitwise_and, g_("n32"), g_("nn"), 128)
+            if k == 0:
+                tc(P, X("nn")[:], g_("nn"), [tp])
+            else:
+                tt(P, X("nn")[:], pm[:, 128:256], OP.add, [PM] + g_("nn"), [tp])
+            if k < 3:
+                MM(["I", tp], [PM], grp(pm[:, 128:256], [(M("I"), P)]), 128)
+                ts(X("msk")[:], P, co(kk), None, OP.is_ge, None, [tp, "co%d" % kk], g_("msk"))
+                tt(X("tq")[:], X("msk")[:], pm[:, 256:384], OP.mult, [PM] + g_("msk"), g_("tq"))
+                tt(X("pp")[:], X("tq")[:], pm[:, 128:256], OP.add, [PM] + g_("tq"), g_("pp"))
+                hn = "h%d" % kk
+                hts = []
+                for q in range(kk + 1, {1: 9, 2: 13, 3: 17}[kk]):
+                    hts.append("%s%s_%d" % (hn, h, q))
+
+                    def mk(o, i, d):
+                        return [("v", cv(64, 1), lambda: g.vector.tensor_scalar(o, i, float(d), None, OP.is_lt)),
+                                ("s", cs(128), lambda: g.scalar.activation(o, i, AF.Sigmoid, scale=-200.0, bias=200.0 * d - 100.0))]
+                    add(mk(X(hn)[:, q - 1:2048:16], X("pp")[:], q - kk), g_("pp", hn), [hts[-1]])
+                scan(X("sc")[:], X(hn)[:], X("dt")[:], OP.add, hts + g_(hn) + ["dt%d%s" % (n, h) for n in range(4)], g_("sc"), 2048)
+                mv = c512(15, 16)
+        gather(4, h)
+        yield
+        for s in (0, 1):
+            o = zb + 5120 * s
+            scan(T.vs[:, o:o + 5120], T.mk5[:], T.zz[:, o:o + 5120], OP.max, ["mk5"] + ["z%d%s%d" % (k, h, s) for k in range(5)], ["vs%d%s" % (s, h)], 5120)
+            it = []
+            for m in range(16):
+                it += grp(pd[:, 64 * m:64 * m + 64], [(M("I"), T.vs[:, o + 5 * m + 4:o + 5 * m + 4 + 80 * 63 + 1:80]), (M("mI"), T.ff[:, b + 64 * s:b + 64 * s + 64])])
+            MM(["I", "mI", "vs%d%s" % (s, h), "ff" + h], [D0, D1], it, 64)
+            act(X("gg")[:], pd[:], AF.Sign, [D0, D1], g_("gg"), 1024, bias=0.5)
+            MM(["cl"] + g_("gg"), [PM], grp(pm[:, 64 * s:64 * s + 64], [(WM("cl", m), X("gg")[:, 64 * m:64 * m + 64]) for m in range(16)]), 64)
+        tc(T.vs[:, zb:zb + 10240:80], T.ff[:, b:b + 128], ["ff" + h, "vs0" + h, "vs1" + h], ["vs0" + h, "vs1" + h])
+        ts(X("fl")[:], pm[:, 0:128], 1.0, None, OP.is_ge, None, [PM], g_("fl"), 128)
+        tt(X("fw")[:], X("fl")[:], X("w3")[:], OP.mult, g_("fl", "w3"), g_("fw"), 256)
+        MM(["BD32"] + g_("fw"), [PU], grp(pu[:, 0:128], [(M("BD32"), X("fw")[:])]), 128)
+        tt(X("cand")[:], X("fw")[:], pu[:, 0:128], OP.is_gt, [PU] + g_("fw"), g_("cand"))
+        MM(["LT"] + g_("cand"), [PU], grp(pu[:, 128:256], [(M("LT"), X("cand")[:])]), 128)
+        tt(win[:], X("cand")[:], pu[:, 128:256], OP.is_gt, [PU] + g_("cand"), g_("win"))
+        if h == "b" and t < 2:
+            MM(["ON", "wina", "winb"], [PM], grp(pm[:, 384:512], [(M("ON"), T.wina[:]), (M("ON"), T.winb[:])]), 128)
+            act(T.junk[:], pm[:, 384:512], AF.Copy, [PM], ["f64", "f32", "ac%d" % (t + 1)], accum_out=T.ac[:, 4 * t + 4:4 * t + 5])
+        MM(["mo"] + g_("win"), [PU], grp(pu[:, 0:8], [(WM("mo", a), win[:, a:128:16]) for a in range(16)]), 8)
+        tt(X("o32")[:], pu[:, 0:8], T.c80[:], OP.add, [PU, "c80"], g_("o32"))
+        ts(X("nk")[:], pu[:, 0:8], 1.0, 4096.0, OP.is_lt, OP.mult, [PU], g_("nk"))
+        tc(X("ofs")[:], X("o32")[:], g_("o32"), g_("ofs"), 64)
+        tc(X("vsel")[:], T.vs[:, zb:zb + 10240].indirect(X("ofs")[:]), ["vs0" + h, "vs1" + h] + g_("ofs"), g_("vsel"), 192)
+        MM(["wl"] + g_("vsel"), [PU], grp(pu[:, 8:16], [(WM("wl", a), X("vsel")[:, a:128:16]) for a in range(16)]), 8)
+        tt(X("nk")[:], X("nk")[:], T.c16[:, b // 16:b // 16 + 8], OP.add, ["c16"] + g_("nk"), g_("nk"))
+        tc(X("q32")[:], pu[:, 8:16], [PU], g_("q32"), 64)
+        ts(X("o32")[:], X("q32")[:], 6, 15, OP.arith_shift_right, OP.bitwise_and, g_("q32"), g_("o32"))
+        tt(X("q32")[:], X("o32")[:], X("nk")[:], OP.add, g_("o32", "nk"), g_("q32"))
+        tc(X("of2")[:], X("q32")[:], g_("q32"), g_("of2"), 64)
+        tc(T.xt[:].indirect(X("of2")[:]), X("vsel")[:], g_("of2", "vsel"), ["x"], 512)
+        MM(["I", "I16", lg, "p1" + h, "p2" + h, "p3" + h, "p4" + h] + g_("win"), [D0, D1],
+           [x for j in range(5) for x in grp(pd[:, 128 * j:128 * j + 128], [(M("I"), X("pt")[:, 128 * j - 128:128 * j] if j else L), (M("I16"), win[:])])], 128)
+        act(wx[:], pd[:, 0:640], AF.Relu, [D0, D1], g_("wx"), 640, bias=-16.0)
+        MM(["LE"] + g_("wx"), [PU], grp(pu[:, 128:256], [(M("LE"), wx[:, 0:128])]), 128)
+        for d in (1, 2, 3, 4):
+            act(X("hn")[:, d:640:5], pu[:, 128:256], AF.Sigmoid, [PU, "hnz" + h], ["+hn" + h], scale=-200.0, bias=200.0 * d - 100.0)
+        scan(X("scn")[:], X("hn")[:], X("rd")[:], OP.add, g_("hn") + ["rd%d%s" % (d, h) for d in range(5)], g_("scn"), 640)
+        NRt = T["nr%d" % t]
+        act(NRt[:, b:b + 128], X("scn")[:, 4:640:5], AF.Copy, g_("scn"), ["nc%d%s" % (t, h)])
+        if t < 2:
+            send(("c" + h, t + 1), NRt[:, b:b + 128], ["nc%d%s" % (t, h)])
+        MM(["B1", "BX32"] + g_("wx", "win"), [D0], [x for j in (1, 2, 3, 4) for x in grp(pd[:, 128 * j - 128:128 * j],
+           [(M("B1"), wx[:, 128 * j:128 * j + 128])] + ([(M("BX32"), win[:])] if j == 4 else []))], 128)
+        ts(X("m4")[:], pd[:, 384:512], co(4), None, OP.is_equal, None, [D0, "co4"], g_("m4"), 128)
+        for j in (1, 2, 3):
+            act(X("ax")[:, 128 * j - 128:128 * j], pd[:, 128 * j - 128:128 * j], AF.Abs, [D0, "co%d" % (4 + j)], ["+ax" + h], bias=co(4 + j))
+        tc(X("z4")[:], T.zz[:, zb:zb + 10240].indirect(X("ofs")[:]), g_("ofs") + ["z%d%s%d" % (k, h, s) for k in range(5) for s in (0, 1)], g_("z4"), 192)
+        tt(X("t4")[:], X("m4")[:], X("scn")[:, 4:640:5], OP.mult, g_("m4", "scn"), g_("t4"), 256)
+        MM(["BW", "B512"] + g_("z4", "t4"), [PU], grp(pu[:, 0:128], [(M("BW"), X("z4")[:]), (M("B512"), X("t4")[:])]), 128)
+        tc(X("n4")[:], pu[:, 0:128], [PU], g_("n4"))
+        ts(X("n5")[:], X("n4")[:], 9, 3, OP.arith_shift_right, OP.bitwise_and, g_("n4"), g_("n5"), 128)
+        tt(X("n4m")[:], X("n5")[:], X("m4")[:], OP.mult, g_("n5", "m4"), g_("n4m"), 256)
+        it = []
+        for j in (1, 2, 3):
+            it += grp(pd[:, 384 + 128 * j:512 + 128 * j], [(M("B1"), wx[:, 128 * j + 128:128 * j + 256]), (M("mB1"), wx[:, 128 * j:128 * j + 128]), (M("mI4"), X("ax")[:, 128 * j - 128:128 * j])])
+        it += grp(pd[:, 896:1024], [(M("I"), L), (M("mB8"), win[:]), (M("I"), T.km1[:])])
+        MM(["B1", "mB1", "mI4", "mB8", "I", "km1", lg] + g_("wx", "ax", "win"), [D1], it, 128)
+        act(X("ex")[:], pd[:, 512:1024], AF.Relu, [D1], g_("ex"), 512)
+        MM(["BQ0", "I"] + g_("wx", "ex", "n4m"), [PU],
+           grp(pu[:, 256:384], [(M("BQ0"), wx[:, 128:256])] + [(M("I"), X("ex")[:, 128 * j:128 * j + 128]) for j in range(4)] + [(M("I"), X("n4m")[:])]), 128)
+        act(NRt[:, 256 + b:384 + b], pu[:, 256:384], AF.Identity, [PU], ["nl%d%s" % (t, h)], bias=1.0)
+        if t < 2:
+            send(("l" + h, t + 1), NRt[:, 256 + b:384 + b], ["nl%d%s" % (t, h)])
+        MM(["I", "kmh", "ff" + h] + g_("vsel"), [PM], grp(pm[:, 384:512], [(M("I"), T.ff[:, b:b + 128]), (M("I"), X("vsel")[:]), (M("I"), T.kmh[:])]), 128)
+        act(X("f1")[:], pm[:, 384:512], AF.Identity, [PM], g_("f1"), scale=0.5, bias=12582912.0)
+        act(T.ff[:, b:b + 128], X("f1")[:], AF.Identity, g_("f1"), ["ff" + h], bias=-12582912.0)
+
+    for t in range(3):
+        for h in "ab":
+            places(t, h)
+        if t == 1:
+            send(("st", 2), T.rec1[:, 512:1024], ["s1"])
+        for part in [stream(t, h) for h in "ab"] * 2:
+            next(part, None)
+    for hb in (0, 1):
+        MM(["I", "x"], ["#pu" + "ab"[hb]], grp(T["pu" + "ab"[hb]][:, 0:128], [(M("I"), T.xt[:, 2048 * hb + a:2048 * hb + 2048:16]) for a in range(16)]), 128)
+        act(T.ysb[:, 128 * hb:128 * hb + 128], T["pu" + "ab"[hb]][:, 0:128], AF.Copy, ["#pu" + "ab"[hb]], ["ysb%d" % hb])
+    dma("y", "o_c", T.yc[:], T.nr2[:, 0:256], ["nc2a", "nc2b"], [])
+    dma("y", "o_l", T.yl[:], T.nr2[:, 256:512], ["nl2a", "nl2b"], [])
+    dma("y", "o_f", T.yf[:], T.ff[:], ["ffa", "ffb"], [])
+    dma("y", "o_s", T.ys[:], T.ysb[:], ["ysb0", "ysb1"], [])
+
+    Q = {"v": g.vector, "s": g.scalar, "t": g.tensor, "g": g, "y": g.sync}
+    cnt = {"v": 0, "s": 0, "t": 0, "g": 0}
+    known = {q: {} for q in Q}
+    lw, rd, bank = {}, {}, {}
+    if not KEEP:
+        KEEP.append(order([(n[0], n[1], n[2], n[3][0]) for n in nodes]))
+    for _, j, a in KEEP[0]:
+        (q, _, f), (_, r, w, kind) = nodes[j][0][a], nodes[j]
+        if kind[0] == "arr":
+            for t in w:
+                lw[t], rd[t] = [(kind[1], kind[2], {})], []
+            continue
+        own, evs = "e_" + q, []
+        for t in r + w:
+            if t[0] == "#":
+                evs += [e for e in bank.get(t, {}).values() if e[0] != own]
+            elif t[0] == "+":
+                evs += rd.get(t[1:], [])
+            else:
+                evs += lw.get(t, []) + (rd.get(t, []) if t in w else [])
+        best = {}
+        for sem, val, clk in evs:
+            if known[q].get(sem, 0) < val and (sem not in best or best[sem][0] < val):
+                best[sem] = (val, clk)
+        for sem, (val, clk) in best.items():
+            if not any(o != sem and best[o][1].get(sem, 0) >= val for o in best):
+                Q[q].wait_ge(T.sem[sem], val)
+        for sem, (val, clk) in best.items():
+            for k, x in list(clk.items()) + [(sem, val)]:
+                known[q][k] = max(known[q].get(k, 0), x)
+        if kind[0] == "send":
+            f()
+            ev = (sends[-1][0], sends[-1][1], dict(known[q]))
+        elif kind[0] == "dma":
+            f().then_inc(T.sem[kind[1]], 16)
+            ev = (kind[1], 16, dict(known[q]))
+        else:
+            cnt[q] += 1
+            f().then_inc(T.sem[own], 1)
+            ev = (own, cnt[q], dict(known[q]))
+            ev[2][own] = cnt[q]
+        for t in set(r + w):
+            if t[0] == "#":
+                bank.setdefault(t, {})[ev[0]] = ev
+            elif t[0] == "+":
+                lw.setdefault(t[1:], []).append(ev)
+            elif t in w:
+                lw[t], rd[t] = [ev], []
+            else:
+                rd[t] = [e for e in rd.get(t, []) if e[0] != ev[0]] + [ev]
+    for q in ("v", "s", "t", "g"):
+        g.wait_ge(T.sem["e_" + q], cnt[q])
+    for s in ("o_c", "o_l", "o_f", "o_s"):
+        g.wait_ge(T.sem[s], 16)
+    for s, n in sends:
+        g.wait_ge(T.sem[s], n)

@@ -6,8 +6,8 @@ SLOTS += ["L%d" % e for e in range(15)]
 SLOT = {n: j for j, n in enumerate(SLOTS)}
 BUF = {"bfloat16": "xt_8192 zz_20480 vs_20480 mk5_5120 wl_2064 cl_2064 mo_2064 ff_256 wtb_16 onef_16 e16_16 tmpm_128 k107_128 km1_128 kmh_128 kd_128 junk_128",
        "float32": "sd_16 jio_16 jt_16 co_24 b8f_8 c80_8 c16_16 ac_16 ysb_256", "int32": "sti_256 tmi_256 tmj_256"}
-BUFH = {"bfloat16": "h0_512 h1_2048 h2_2048 h3_2048 t0_512 dt_2048 sc_2048 rd_640 hn_640 scn_640 gg_1024 c5_128 pt_512 pp_128 "
-                    "msk_128 tq_128 w3_128 fl_128 fw_128 cand_128 win_128 vsel_128 z4_128 wx_640 ax_384 ex_512 m4_128 t4_128 n4m_128",
+BUFH = {"bfloat16": "h0_512 h1_2048 h2_2048 h3_2048 t0_512 dt_2048 sc_2048 rd_640 hn_640 scn_640 gg_1024 c5_128 pt_896 pp_256 "
+                    "msk_256 w3_128 fl_128 fw_128 cand_128 win_128 vsel_128 z4_128 wx_640 ax_384 ex_512 m4_128 t4_128 n4m_128",
         "float32": "nk_8 f1_128", "int32": "s32_128 x32_128 r32_128 n32_128 nn_128 n4_128 n5_128 o32_8 q32_8", "uint16": "offs_128 ofs_8 of2_8"}
 
 
@@ -103,7 +103,7 @@ def order(nodes):
             c.append((best, j))
         e, j = min(c, key=lambda x: (x[0][1], -prio[x[1]]))
         t0, q0 = e[1], e[3]
-        e, j = max([x for x in c if x[0][3] == q0 and x[0][1] <= t0 + 100], key=lambda x: (prio[x[1]], -x[1]))
+        e, j = max([x for x in c if x[0][3] == q0 and x[0][1] <= t0 + 30], key=lambda x: (prio[x[1]], -x[1]))
         fin, s, a, q = e
         ready.remove(j)
         end[j], qof[j] = fin, q
@@ -167,8 +167,18 @@ def rank_program(g, core, T, topo):
     def act(out, in_, func, r, w, n=128, k=1, **kw):
         add([("s", cs(n, k), lambda: g.scalar.activation(out, in_, func, **kw))], r, w)
 
+    def flex(out, in_, func, r, w, n, v, **kw):
+        add([("s", cs(n), lambda: g.scalar.activation(out, in_, func, **kw)),
+             ("v", cv(n, 1), lambda: g.vector.tensor_scalar(out, in_, *v) if v else g.vector.tensor_copy(out, in_))], r, w)
+
     def gp(meth, r, w, *a, **kw):
         add([("g", 350, lambda: {"iota": g.iota, "sel": g.affine_select}[meth](*a, **kw))], r, w)
+
+    def fill(nm, n, v, tag):
+        add([("g", 150 + n * 1.9, lambda: g.iota(T[nm][:], [[0, n]], v, 0, allow_small_or_imprecise_dtypes=True))], [], [tag])
+
+    def cpy(out, in_, r, w):
+        add([("g", 420, lambda: g.affine_select(out, in_, [[0, 128]], OP.is_ge, 0.0, 1, 0))], r, w)
 
     def MM(r, w, items, ns):
         def f():
@@ -195,9 +205,10 @@ def rank_program(g, core, T, topo):
     dma("y", "ld_x", T.xt[:, 0:4096], T.x[:], [], ["x"], 8000)
     dma("s", "ld_ch", T.rec0[:, 0:256], T.ch[:], [], ["c0a", "c0b"])
     dma("s", "ld_fl", T.ff[:], T.fl[:], [], ["ffa", "ffb"])
-    ms(M("ON"), 1.0, ["ON"]); ms(T.onef[:], 1.0, ["onef"])
-    for nm in ("wl", "cl", "mo"):
-        ms(T[nm][:], 0.0, [nm + "0"], 1032)
+    ms(M("ON"), 1.0, ["ON"]); ms(T.onef[:], 1.0, ["onef"]); ms(T.wl[:], 0.0, ["wl0"], 1032)
+    for nm in ("h1a", "h1b", "h2a", "h2b"):
+        fill(nm, 2048, 1, nm)
+    fill("mk5", 5120, 1, "mk5"); fill("cl", 2064, 0, "cl0"); fill("mo", 2064, 0, "mo0")
     for nm, st in (("jio", [[1, 16]]), ("c80", [[1280, 8]]), ("c16", [[256, 16]])):
         gp("iota", [], [nm], T[nm][:], st, 0, 0, allow_small_or_imprecise_dtypes=True)
     gp("sel", ["ON"], ["I"], M("I"), M("ON"), [[-1, 128]], OP.is_equal, 0.0, 0, 1)
@@ -226,6 +237,7 @@ def rank_program(g, core, T, topo):
     ts(co(10), co(0), 80.0, None, OP.mult, None, ["co0"], ["co10"])
     ts(co(11), co(0), 16.0, None, OP.mult, None, ["co0"], ["co11"])
     ts(co(12), T.e16[:, 0:1], 1.0, None, OP.mult, None, ["e16"], ["co12"])
+    ts(co(14), T.e16[:, 4:5], 0.03125, None, OP.mult, None, ["e16"], ["co14"])
     ts(co(13), T.e16[:, 0:1], -1.0, 1.0, OP.mult, OP.add, ["e16"], ["co13"])
     ts(T.c80[:], T.c80[:], co(10), None, OP.add, None, ["co10", "c80"], ["c80"])
     ts(T.c16[:], T.c16[:], co(11), None, OP.add, None, ["co11", "c16"], ["c16"])
@@ -237,48 +249,45 @@ def rank_program(g, core, T, topo):
         ts(T.wl[:, sl], T.onef[:], co(9), colb, OP.mult, OP.mult, ["onef", "co9", "b8f", "wl0"], ["+wl"])
         ts(T.cl[:, sl], T.onef[:], colb, None, OP.mult, None, ["onef", "b8f", "cl0"], ["+cl"])
         ts(T.mo[:, sl], T.onef[:], co(8), colb, OP.mult, OP.mult, ["onef", "co8", "b8f", "mo0"], ["+mo"])
-    tt(T.sd[:, 1:15], T.e16[:, 1:15], T.e16[:, 2:16], OP.subtract, ["e16"], ["+sd"])
-    tc(T.sd[:, 15:16], T.e16[:, 15:16], ["e16"], ["+sd"])
-    tc(T.sd[:, 0:1], T.e16[:, 0:1], ["e16"], ["+sd"])
+    tt(T.jt[:, 1:15], T.e16[:, 1:15], T.e16[:, 2:16], OP.subtract, ["e16", "co0"], ["+jd"])
+    tc(T.jt[:, 15:16], T.e16[:, 15:16], ["e16", "co0"], ["+jd"])
+    tc(T.jt[:, 0:1], T.e16[:, 0:1], ["e16", "co0"], ["+jd"])
+    ts(T.sd[:], T.jt[:], 0.03125, None, OP.mult, None, ["jd"], ["sd"])
 
-    def mat(dst, src, f, f2=None, r2=()):
-        ts(M(dst), M(src), f, f2, OP.mult, None if f2 is None else OP.mult, [src] + list(r2), [dst])
+    def mat(dst, src, f, r2=()):
+        add([("v", cv(64, 1), lambda: g.vector.tensor_scalar(M(dst), M(src), f, None, OP.mult)),
+             ("s", cs(128), lambda: g.scalar.activation(M(dst), M(src), AF.Copy, scale=f))], [src] + list(r2), [dst])
 
     for nm, f in (("I512", 512.0), ("I101", 101.0), ("I64", 64.0), ("I32", 32.0), ("mI", -1.0), ("I16", 16.0), ("mI4", -4.0)):
         mat(nm, "I", f)
-    mat("T0", "B1", T.sd[:, 0:1], 0.03125, ["sd"])
+    mat("T0", "B1", T.sd[:, 0:1], ["sd"])
     for e in range(4):
         nm = "T%d" % e
         if e:
             ms(M(nm), 0.0, [nm])
         o = SLOT[nm] * 128
-        sc = T.sd[:, e + 1:e + 2] if e < 3 else T.e16[:, 4:5]
-        ts(T.mats[:, o:o + 113:16], T.mats[:, b8:b8 + 113:16], sc, 0.03125, OP.mult, OP.mult, ["B1", "sd", "e16"], [nm])
-    mat("DG0", "I", co(13), None, ["co13"]); mat("DG3", "I", co(12), None, ["co12"])
+        ts(T.mats[:, o:o + 113:16], T.mats[:, b8:b8 + 113:16], T.sd[:, e + 1:e + 2] if e < 3 else co(14), None, OP.mult, None, ["B1", "sd", "co14"], [nm])
+    mat("DG0", "I", co(13), ["co13"]); mat("DG3", "I", co(12), ["co12"])
     for nm, v in (("kd", -215.0 / 64), ("k107", 107.5), ("km1", -1.0), ("kmh", -0.5)):
         ms(T[nm][:], v, [nm])
     for e in range(15):
-        mat("L%d" % e, "B1", T.sd[:, e + 1:e + 2], 0.03125, ["sd"])
+        mat("L%d" % e, "B1", T.sd[:, e + 1:e + 2], ["sd"])
     for nm, f in (("mB1", -1.0), ("mB8", -8.0), ("BD32", 0.03125), ("B512", 512.0), ("BX32", 32.0)):
         mat(nm, "B1", f)
-    mat("BW", "B1", co(9), None, ["co9"])
+    mat("BW", "B1", co(9), ["co9"])
     for d in range(4):
         s0 = "S%d" % d if d else "I"
         tt(M("E%d" % d), M(s0), M("S%d" % (d + 1)), OP.subtract, [s0, "S%d" % (d + 1)], ["E%d" % d], 256)
     ms(M("BQ0"), 0.0, ["BQ0"])
     o = SLOT["BQ0"] * 128
     tc(T.mats[:, o:o + 113:16], T.mats[:, b8:b8 + 113:16], ["B1"], ["BQ0"])
-    ms(T.mk5[:], 1.0, ["mk5"], 2560)
     ms(T.mk5[:, 0:5120:5], 0.0, ["mk5"], 1024)
     ms(T.ac[:, 0:1], 0.0, ["ac0"])
     for h in "ab":
-        ms(T["h0" + h][:], 0.0, ["h0z" + h], 256); ms(T["hn" + h][:], 0.0, ["hnz" + h], 320)
+        ms(T["msk" + h][:], 0.0, ["mskz" + h], 128); ms(T["h0" + h][:], 0.0, ["h0z" + h], 256); ms(T["hn" + h][:], 0.0, ["hnz" + h], 320)
         for k in (1, 2, 3):
-            nm = "h%d%s" % (k, h)
-            if k < 3:
-                ms(T[nm][:], 1.0, [nm], 1024)
             for e in range(k):
-                ms(T[nm][:, e:2048:16], 0.0, [nm])
+                ms(T["h%d%s" % (k, h)][:, e:2048:16], 0.0, ["h%d%s" % (k, h)])
 
     sends = []
 
@@ -301,10 +310,11 @@ def rank_program(g, core, T, topo):
         tc(T["offs" + h][:], T["r32" + h][:], ["r32" + h], ["off" + h])
 
     def gather(k, h):
-        for s in (0, 1):
-            c0 = 128 * (h == "b") + 64 * s
-            act(T.zz[:, 80 * c0 + k:80 * (c0 + 64) - 4 + k:5], T.xt[:, 0:4096].indirect(T["offs" + h][:, 64 * s:64 * s + 64]), AF.Copy,
-                ["x", "off" + h], ["z%d%s%d" % (k, h, s)], 1024, 1.5)
+        w = 64 if k == 4 else 128
+        for s in range(128 // w):
+            c0 = 128 * (h == "b") + w * s
+            act(T.zz[:, 80 * c0 + k:80 * (c0 + w) - 4 + k:5], T.xt[:, 0:4096].indirect(T["offs" + h][:, w * s:w * s + w]), AF.Copy,
+                ["x", "off" + h], ["z%d%s%d" % (k, h, s)], 16 * w, 1.5)
 
     def stream(t, h):
         b = 128 * (h == "b")
@@ -320,10 +330,14 @@ def rank_program(g, core, T, topo):
         for e in range(4):
             MM(["T%d" % e, "DG0", "DG3", "kd", cg], [D0],
                grp(pd[:, e:509 + e:4], [(M("T%d" % e), C)] + ([(M("DG%d" % e), T.kd[:])] if e in (0, 3) else [])), 128)
-        act(X("t0")[:], pd[:, 0:512], AF.Copy, [D0], g_("t0"), 512)
-        ts(X("pp")[:], L, -1.0, co(12), OP.add, OP.mult, [lg, "co12"], g_("pp"))
+        flex(X("t0")[:], pd[:, 0:512], AF.Copy, [D0], g_("t0"), 512, None)
+        ppv = X("pp")[:, 1:256:2]
+        pts = [X("pt")[:, 256 * j + 1:256 * j + 256:2] for j in range(3)] + [X("pt")[:, 768:896]]
+        for j in range(3):
+            cpy(X("pt")[:, 256 * j:256 * j + 255:2], L, [lg], ["lp%d%s" % (j + 1, h)])
+        ts(ppv, L, -1.0, co(12), OP.add, OP.mult, [lg, "co12"], g_("pp"))
         for e in (1, 2, 3):
-            ts(X("h0")[:, e:512:4], X("pp")[:], float(e), None, OP.is_lt, None, g_("pp", "h0z"), ["+h0" + h])
+            ts(X("h0")[:, e:512:4], ppv, float(e), None, OP.is_lt, None, g_("pp", "h0z"), ["+h0" + h])
         scan(X("sc")[:, 0:512], X("h0")[:], X("t0")[:], OP.add, g_("h0", "t0"), g_("sc"), 512)
 
         def c512(y, ys):
@@ -333,7 +347,6 @@ def rank_program(g, core, T, topo):
             return i
 
         mv = c512(3, 4)
-        MM(["I", lg], [PM], grp(pm[:, 256:384], [(M("I"), L)]), 128)
         for n in (0, 1):
             it = []
             for hb in (0, 1):
@@ -343,10 +356,10 @@ def rank_program(g, core, T, topo):
             MM(["L%d" % e for e in range(15)] + ["I", "kd", cg], [D0, D1], it, 32)
             for hb in (0, 1):
                 c0 = 1024 * n + 512 * hb
-                act(X("dt")[:, c0:c0 + 512], pd[:, 512 * hb:512 * hb + 512], AF.Copy, [D1 if hb else D0], ["dt%d%s" % (2 * n + hb, h)], 512)
+                flex(X("dt")[:, c0:c0 + 512], pd[:, 512 * hb:512 * hb + 512], AF.Copy, [D1 if hb else D0], ["dt%d%s" % (2 * n + hb, h)], 512, None)
         MM(["E0", "E1", "E2", "E3", "S4", cg], [D0, D1], [x for d in range(5) for x in grp(pd[:, 128 * d:128 * d + 128], [(M("E%d" % d if d < 4 else "S4"), C)])], 128)
         for d in range(5):
-            act(X("rd")[:, d:640:5], pd[:, 128 * d:128 * d + 128], AF.Copy, [D1 if d == 4 else D0], ["rd%d%s" % (d, h)])
+            flex(X("rd")[:, d:640:5], pd[:, 128 * d:128 * d + 128], AF.Copy, [D1 if d == 4 else D0], ["rd%d%s" % (d, h)], 128, None)
         act(X("w3")[:], L, AF.Sigmoid, [lg], g_("w3"), scale=3.4657359027997265, bias=-41.58883083359672)
 
         zb = 80 * b
@@ -354,7 +367,7 @@ def rank_program(g, core, T, topo):
             kk = k + 1
             gather(k, h)
             U, U2 = pu[:, 0:128], pd[:, 0:128]
-            zt = ["wl", "z%d%s0" % (k, h), "z%d%s1" % (k, h)]
+            zt = ["wl", "z%d%s0" % (k, h)]
             us = [(WM("wl", m), T.zz[:, zb + 5 * m + k:zb + 5 * m + k + 80 * 127 + 1:80]) for m in range(16)]
             MM(zt, [PU], grp(U, us), 128)
             tt(X("x32")[:], U, mv, OP.mult, [PU] + g_("sc"), g_("x32"))
@@ -364,7 +377,7 @@ def rank_program(g, core, T, topo):
             tt(X("r32")[:], X("s32")[:], U2, OP.add, [D0] + g_("s32"), g_("r32"))
             ts(X("s32")[:], X("r32")[:], 4095, None, OP.bitwise_and, None, g_("r32"), g_("s32"), 128)
             tc(X("offs")[:], X("s32")[:], g_("s32"), ["off" + h])
-            P = X("pt")[:, 128 * k:128 * kk]
+            P = pts[k]
             tp = "p%d%s" % (kk, h)
             ts(X("nn")[:], X("n32")[:], 9, 3, OP.arith_shift_right, OP.bitwise_and, g_("n32"), g_("nn"), 128)
             if k == 0:
@@ -373,9 +386,8 @@ def rank_program(g, core, T, topo):
                 tt(P, X("nn")[:], pm[:, 128:256], OP.add, [PM] + g_("nn"), [tp])
             if k < 3:
                 MM(["I", tp], [PM], grp(pm[:, 128:256], [(M("I"), P)]), 128)
-                ts(X("msk")[:], P, co(kk), None, OP.is_ge, None, [tp, "co%d" % kk], g_("msk"))
-                tt(X("tq")[:], X("msk")[:], pm[:, 256:384], OP.mult, [PM] + g_("msk"), g_("tq"))
-                tt(X("pp")[:], X("tq")[:], pm[:, 128:256], OP.add, [PM] + g_("tq"), g_("pp"))
+                ts(X("msk")[:, 1:256:2], P, co(kk), None, OP.is_ge, None, [tp, "co%d" % kk] + g_("mskz"), g_("msk"))
+                scan(X("pp")[:], X("msk")[:], X("pt")[:, 256 * k:256 * kk], OP.add, [tp, "lp%d%s" % (kk, h)] + g_("msk", "mskz"), g_("pp"), 256)
                 hn = "h%d" % kk
                 hts = []
                 for q in range(kk + 1, {1: 9, 2: 13, 3: 17}[kk]):
@@ -384,22 +396,22 @@ def rank_program(g, core, T, topo):
                     def mk(o, i, d):
                         return [("v", cv(64, 1), lambda: g.vector.tensor_scalar(o, i, float(d), None, OP.is_lt)),
                                 ("s", cs(128), lambda: g.scalar.activation(o, i, AF.Sigmoid, scale=-200.0, bias=200.0 * d - 100.0))]
-                    add(mk(X(hn)[:, q - 1:2048:16], X("pp")[:], q - kk), g_("pp", hn), [hts[-1]])
+                    add(mk(X(hn)[:, q - 1:2048:16], ppv, q - kk), g_("pp", hn), [hts[-1]])
                 scan(X("sc")[:], X(hn)[:], X("dt")[:], OP.add, hts + g_(hn) + ["dt%d%s" % (n, h) for n in range(4)], g_("sc"), 2048)
                 mv = c512(15, 16)
         gather(4, h)
         yield
         for s in (0, 1):
             o = zb + 5120 * s
-            scan(T.vs[:, o:o + 5120], T.mk5[:], T.zz[:, o:o + 5120], OP.max, ["mk5"] + ["z%d%s%d" % (k, h, s) for k in range(5)], ["vs%d%s" % (s, h)], 5120)
+            scan(T.vs[:, o:o + 5120], T.mk5[:], T.zz[:, o:o + 5120], OP.max, ["mk5", "z4%s%d" % (h, s)] + ["z%d%s0" % (k, h) for k in range(4)], ["vs%d%s" % (s, h)], 5120)
             it = []
             for m in range(16):
                 it += grp(pd[:, 64 * m:64 * m + 64], [(M("I"), T.vs[:, o + 5 * m + 4:o + 5 * m + 4 + 80 * 63 + 1:80]), (M("mI"), T.ff[:, b + 64 * s:b + 64 * s + 64])])
             MM(["I", "mI", "vs%d%s" % (s, h), "ff" + h], [D0, D1], it, 64)
             act(X("gg")[:], pd[:], AF.Sign, [D0, D1], g_("gg"), 1024, bias=0.5)
             MM(["cl"] + g_("gg"), [PM], grp(pm[:, 64 * s:64 * s + 64], [(WM("cl", m), X("gg")[:, 64 * m:64 * m + 64]) for m in range(16)]), 64)
-        tc(T.vs[:, zb:zb + 10240:80], T.ff[:, b:b + 128], ["ff" + h, "vs0" + h, "vs1" + h], ["vs0" + h, "vs1" + h])
-        ts(X("fl")[:], pm[:, 0:128], 1.0, None, OP.is_ge, None, [PM], g_("fl"), 128)
+        cpy(T.vs[:, zb:zb + 10240:80], T.ff[:, b:b + 128], ["ff" + h, "vs0" + h, "vs1" + h], ["vs0" + h, "vs1" + h])
+        flex(X("fl")[:], pm[:, 0:128], AF.Sigmoid, [PM], g_("fl"), 128, (1.0, None, OP.is_ge), scale=200.0, bias=-100.0)
         tt(X("fw")[:], X("fl")[:], X("w3")[:], OP.mult, g_("fl", "w3"), g_("fw"), 256)
         MM(["BD32"] + g_("fw"), [PU], grp(pu[:, 0:128], [(M("BD32"), X("fw")[:])]), 128)
         tt(X("cand")[:], X("fw")[:], pu[:, 0:128], OP.is_gt, [PU] + g_("fw"), g_("cand"))
@@ -421,14 +433,14 @@ def rank_program(g, core, T, topo):
         tc(X("of2")[:], X("q32")[:], g_("q32"), g_("of2"), 64)
         tc(T.xt[:].indirect(X("of2")[:]), X("vsel")[:], g_("of2", "vsel"), ["x"], 512)
         MM(["I", "I16", lg, "p1" + h, "p2" + h, "p3" + h, "p4" + h] + g_("win"), [D0, D1],
-           [x for j in range(5) for x in grp(pd[:, 128 * j:128 * j + 128], [(M("I"), X("pt")[:, 128 * j - 128:128 * j] if j else L), (M("I16"), win[:])])], 128)
-        act(wx[:], pd[:, 0:640], AF.Relu, [D0, D1], g_("wx"), 640, bias=-16.0)
+           [x for j in range(5) for x in grp(pd[:, 128 * j:128 * j + 128], [(M("I"), pts[j - 1] if j else L), (M("I16"), win[:])])], 128)
+        flex(wx[:], pd[:, 0:640], AF.Relu, [D0, D1], g_("wx"), 640, (-16.0, 0.0, OP.add, OP.max), bias=-16.0)
         MM(["LE"] + g_("wx"), [PU], grp(pu[:, 128:256], [(M("LE"), wx[:, 0:128])]), 128)
         for d in (1, 2, 3, 4):
-            act(X("hn")[:, d:640:5], pu[:, 128:256], AF.Sigmoid, [PU, "hnz" + h], ["+hn" + h], scale=-200.0, bias=200.0 * d - 100.0)
+            flex(X("hn")[:, d:640:5], pu[:, 128:256], AF.Sigmoid, [PU, "hnz" + h], ["+hn" + h], 128, (float(d), None, OP.is_lt), scale=-200.0, bias=200.0 * d - 100.0)
         scan(X("scn")[:], X("hn")[:], X("rd")[:], OP.add, g_("hn") + ["rd%d%s" % (d, h) for d in range(5)], g_("scn"), 640)
         NRt = T["nr%d" % t]
-        act(NRt[:, b:b + 128], X("scn")[:, 4:640:5], AF.Copy, g_("scn"), ["nc%d%s" % (t, h)])
+        flex(NRt[:, b:b + 128], X("scn")[:, 4:640:5], AF.Copy, g_("scn"), ["nc%d%s" % (t, h)], 64, None)
         if t < 2:
             send(("c" + h, t + 1), NRt[:, b:b + 128], ["nc%d%s" % (t, h)])
         MM(["B1", "BX32"] + g_("wx", "win"), [D0], [x for j in (1, 2, 3, 4) for x in grp(pd[:, 128 * j - 128:128 * j],
@@ -436,7 +448,7 @@ def rank_program(g, core, T, topo):
         ts(X("m4")[:], pd[:, 384:512], co(4), None, OP.is_equal, None, [D0, "co4"], g_("m4"), 128)
         for j in (1, 2, 3):
             act(X("ax")[:, 128 * j - 128:128 * j], pd[:, 128 * j - 128:128 * j], AF.Abs, [D0, "co%d" % (4 + j)], ["+ax" + h], bias=co(4 + j))
-        tc(X("z4")[:], T.zz[:, zb:zb + 10240].indirect(X("ofs")[:]), g_("ofs") + ["z%d%s%d" % (k, h, s) for k in range(5) for s in (0, 1)], g_("z4"), 192)
+        tc(X("z4")[:], T.zz[:, zb:zb + 10240].indirect(X("ofs")[:]), g_("ofs") + ["z4%s1" % h] + ["z%d%s0" % (k, h) for k in range(5)], g_("z4"), 192)
         tt(X("t4")[:], X("m4")[:], X("scn")[:, 4:640:5], OP.mult, g_("m4", "scn"), g_("t4"), 256)
         MM(["BW", "B512"] + g_("z4", "t4"), [PU], grp(pu[:, 0:128], [(M("BW"), X("z4")[:]), (M("B512"), X("t4")[:])]), 128)
         tc(X("n4")[:], pu[:, 0:128], [PU], g_("n4"))
@@ -447,10 +459,10 @@ def rank_program(g, core, T, topo):
             it += grp(pd[:, 384 + 128 * j:512 + 128 * j], [(M("B1"), wx[:, 128 * j + 128:128 * j + 256]), (M("mB1"), wx[:, 128 * j:128 * j + 128]), (M("mI4"), X("ax")[:, 128 * j - 128:128 * j])])
         it += grp(pd[:, 896:1024], [(M("I"), L), (M("mB8"), win[:]), (M("I"), T.km1[:])])
         MM(["B1", "mB1", "mI4", "mB8", "I", "km1", lg] + g_("wx", "ax", "win"), [D1], it, 128)
-        act(X("ex")[:], pd[:, 512:1024], AF.Relu, [D1], g_("ex"), 512)
+        flex(X("ex")[:], pd[:, 512:1024], AF.Relu, [D1], g_("ex"), 512, (0.0, None, OP.max))
         MM(["BQ0", "I"] + g_("wx", "ex", "n4m"), [PU],
            grp(pu[:, 256:384], [(M("BQ0"), wx[:, 128:256])] + [(M("I"), X("ex")[:, 128 * j:128 * j + 128]) for j in range(4)] + [(M("I"), X("n4m")[:])]), 128)
-        act(NRt[:, 256 + b:384 + b], pu[:, 256:384], AF.Identity, [PU], ["nl%d%s" % (t, h)], bias=1.0)
+        flex(NRt[:, 256 + b:384 + b], pu[:, 256:384], AF.Identity, [PU], ["nl%d%s" % (t, h)], 128, (1.0, None, OP.add), bias=1.0)
         if t < 2:
             send(("l" + h, t + 1), NRt[:, 256 + b:384 + b], ["nl%d%s" % (t, h)])
         MM(["I", "kmh", "ff" + h] + g_("vsel"), [PM], grp(pm[:, 384:512], [(M("I"), T.ff[:, b:b + 128]), (M("I"), X("vsel")[:]), (M("I"), T.kmh[:])]), 128)

from concourse.mybir import AluOpType as OP, AxisListType, ActivationFunctionType as AF

SLOTS = ["I", "B1", "ON", "LT", "LE", "S1", "S2", "S3", "S4", "E0", "E1", "E2", "E3", "I32", "I512", "I101", "I64", "mI",
         "I16", "mB1", "mI4", "mB8", "BD32", "B512", "BX32", "BW", "BQ0", "T0", "T1", "T2", "T3", "DG0", "DG3"]
SLOTS += ["L%d" % e for e in range(15)]
SLOT = {n: j for j, n in enumerate(SLOTS)}
BUF = {"bfloat16": "xt_8192 zz_20480 vs_20480 mk5_5120 wl_2064 cl_2064 mo_2064 ff_256 wtb_16 onef_16 e16_16 tmpm_128 k107_128 km1_128 kmh_128 kd_128 junk_128",
       "float32": "sd_16 jio_16 jt_16 co_24 b8f_8 c80_8 c16_16 ac_16 ysb_256", "int32": "sti_256 tmi_256 tmj_256"}
BUFH = {"bfloat16": "h0_512 h1_2048 h2_2048 h3_2048 t0_512 dt_2048 sc_2048 rd_640 hn_640 scn_640 gg_1024 c5_128 pt_896 pp_256 "
                    "msk_256 w3_128 fl_128 fw_128 cand_128 win_128 vsel_128 z4_128 wx_640 ax_384 ex_512 m4_128 t4_128 n4m_128",
        "float32": "nk_8 f1_128", "int32": "s32_128 x32_128 r32_128 n32_128 nn_128 n4_128 n5_128 o32_8 q32_8", "uint16": "offs_128 ofs_8 of2_8"}


def _bufs():
    out = {"mats": ("sbuf", [128, len(SLOTS) * 128], "bfloat16")}
    for table, hs in ((BUF, ("",)), (BUFH, ("a", "b"))):
        for dt, names in table.items():
            for s in names.split():
                nm, n = s.split("_")
                for h in hs:
                    out[nm + h] = ("sbuf", [128, int(n)], dt)
    for t in range(3):
        out["rec%d" % t] = ("sbuf", [128, 1024], "bfloat16")
        out["nr%d" % t] = ("sbuf", [128, 512], "bfloat16")
    for h in "ab":
        out["pu" + h] = out["pm" + h] = ("psum", [128, 512], "float32")
        out["pd" + h] = ("psum", [128, 1024], "float32")
    return out


SCRATCH = _bufs()
MSG = [("st", 1), ("st", 2)] + [(k + h, t) for t in (1, 2) for h in "ab" for k in "cl"]
COLS = {"st": (512, 1024), "ca": (0, 128), "cb": (128, 256), "la": (256, 384), "lb": (384, 512)}
SEMAPHORES = ["e_v", "e_s", "e_t", "e_g"] + ["ld_" + n for n in ("st", "sp", "wt", "x", "ch", "fl")] + ["o_c", "o_l", "o_f", "o_s"]
SEMAPHORES += [p + "%s%d" % m for m in MSG for p in ("a_", "b_")]
KEEP = []


def nbits(m):
    return bin(m).count("1")


def relays(src, dst, topo):
    if topo.may_write(src, dst):
        return []
    own = [c for c in topo.cores_of(src) if c != src and topo.may_write(c, dst)]
    return sorted(own, key=lambda c: (topo.die(c) != topo.die(src), c))


def via(msg, src, dst, topo):
    own = relays(src, dst, topo)
    return own[(msg[0][-1] == "a") % len(own)] if own else None


def cv(n, k):
    return 55 + max(64, n * k) * 0.95


def cs(n, k=1):
    return 65 + n * k * 0.95


def order(nodes):
    n = len(nodes)
    pred, succ, lw, rd = [[] for _ in range(n)], [[] for _ in range(n)], {}, {}
    for j, (alts, r, w, _) in enumerate(nodes):
        ws = w + [t for t in r if t[0] == "#"]
        ps = set()
        for t in r + ws:
            ps.update(lw.get(t, []) if t[0] != "+" else rd.get(t[1:], []))
        for t in ws:
            ps.update(rd.get(t, []))
        for t in r:
            rd.setdefault(t, []).append(j)
        for t in ws:
            if t[0] == "+":
                lw.setdefault(t[1:], []).append(j)
            else:
                lw[t], rd[t] = [j], []
        pred[j] = sorted(ps - {j})
        for p in pred[j]:
            succ[p].append(j)
    prio = [0.0] * n
    for j in range(n - 1, -1, -1):
        prio[j] = nodes[j][0][0][1] + 80 + max([prio[x] for x in succ[j]] + [0])
    for j in range(n):
        if any(t[-1] == "a" for t in nodes[j][2]):
            prio[j] += 3000
    left = [len(p) for p in pred]
    ready = [j for j in range(n) if not left[j]]
    free, end, qof, out = {}, [0.0] * n, [None] * n, []
    while ready:
        c = []
        for j in ready:
            best = None
            for a, alt in enumerate(nodes[j][0]):
                q, cost = alt[0], alt[1]
                s = free.get(q, 0.0) if q != "n" else 0.0
                for p in pred[j]:
                    s = max(s, end[p] + (20 if qof[p] == q else 80))
                if best is None or s + cost < best[0]:
                    best = (s + cost, s, a, q)
            c.append((best, j))
        e, j = min(c, key=lambda x: (x[0][1], -prio[x[1]]))
        t0, q0 = e[1], e[3]
        e, j = max([x for x in c if x[0][3] == q0 and x[0][1] <= t0 + 30], key=lambda x: (prio[x[1]], -x[1]))
        fin, s, a, q = e
        ready.remove(j)
        end[j], qof[j] = fin, q
        free[q] = s + 70 if nodes[j][3] == "dma" else fin
        out.append((s, j, a))
        for x in succ[j]:
            left[x] -= 1
            if not left[x]:
                ready.append(x)
    return out


def rank_program(g, core, T, topo):
    N = len(T.cores)
    rank = T.rank_of(core)

    def put(msg, src_ap, dst):
        a, b = COLS[msg[0]]
        rid, pid = topo.addr(dst, core)
        m = topo.mask(core, dst)
        g.remote_dma(T["rec%d" % msg[1]][:, a:b], src_ap, T.sem["a_%s%d" % msg], T.sem["b_%s%d" % msg], pid, rid, m)
        return nbits(m)

    if rank is None:
        for r in range(N):
            src, dst = T.cores[r], T.cores[(r + 1) % N]
            sent = []
            for msg in [x for x in MSG if via(x, src, dst, topo) == core]:
                a, b = COLS[msg[0]]
                g.wait_ge(T.sem["a_%s%d" % msg], nbits(topo.mask(src, core)))
                sent.append((msg, put(msg, T["rec%d" % msg[1]][:, a:b], dst)))
            for msg, n in sent:
                g.wait_ge(T.sem["b_%s%d" % msg], n)
        return

    nxt, prv = T.cores[(rank + 1) % N], T.cores[(rank - 1) % N]
    nodes = []

    def add(alts, r, w, kind="op"):
        nodes.append((alts, list(r), list(w), kind))

    def vop(meth, cost, r, w, *a):
        add([("v", cost, lambda: {"tt": g.vector.tensor_tensor, "ts": g.vector.tensor_scalar, "tc": g.vector.tensor_copy, "ms": g.vector.memset,
                                  "sc": g.vector.tensor_tensor_scan, "tr": g.vector.tensor_reduce}[meth](*a))], r, w)

    def tt(out, a, b, op, r, w, c=128):
        vop("tt", cv(c, 1), r, w, out, a, b, op)

    def ts(out, a, s1, s2, o1, o2, r, w, c=64):
        vop("ts", cv(c, 1), r, w, *((out, a, s1, s2, o1) if o2 is None else (out, a, s1, s2, o1, o2)))

    def tc(out, a, r, w, c=128):
        vop("tc", cv(c, 1), r, w, out, a)

    def ms(ap, val, w, c=64):
        vop("ms", cv(c, 1), [], w, ap, val)

    def scan(out, a, b, o1, r, w, n):
        vop("sc", cv(n, 0.5), r, w, out, a, b, 0.0, OP.mult, o1)

    def act(out, in_, func, r, w, n=128, k=1, **kw):
        add([("s", cs(n, k), lambda: g.scalar.activation(out, in_, func, **kw))], r, w)

    def flex(out, in_, func, r, w, n, v, **kw):
        add([("s", cs(n), lambda: g.scalar.activation(out, in_, func, **kw)),
             ("v", cv(n, 1), lambda: g.vector.tensor_scalar(out, in_, *v) if v else g.vector.tensor_copy(out, in_))], r, w)

    def gp(meth, r, w, *a, **kw):
        add([("g", 350, lambda: {"iota": g.iota, "sel": g.affine_select}[meth](*a, **kw))], r, w)

    def fill(nm, n, v, tag):
        add([("g", 150 + n * 1.9, lambda: g.iota(T[nm][:], [[0, n]], v, 0, allow_small_or_imprecise_dtypes=True))], [], [tag])

    def cpy(out, in_, r, w):
        add([("g", 420, lambda: g.affine_select(out, in_, [[0, 128]], OP.is_ge, 0.0, 1, 0))], r, w)

    def MM(r, w, items, ns):
        def f():
            for o, l, x, s0, s1 in items:
                i = g.tensor.matmul(o, l, x, s0, s1)
            return i
        add([("t", 60 + 0.45 * max(64, ns) * len(items), f)], r, w)

    def grp(out, pairs):
        return [(out, l, x, j == 0, j == len(pairs) - 1) for j, (l, x) in enumerate(pairs)]

    def M(n):
        return T.mats[:, SLOT[n] * 128:SLOT[n] * 128 + 128]

    def WM(n, m):
        return T[n][:, 128 * m:128 * m + 128]

    def dma(q, sem, out, in_, r, w, cost=2600):
        add([(q, cost, lambda: {"y": g.sync, "s": g.scalar}[q].dma_start(out, in_))], r, w, ("dma", sem, 16))

    dma("s", "ld_st", T.sti[:], T.st[:], [], ["sti"])
    dma("s", "ld_sp", T.rec0[:, 256:512], T.sp[:], [], ["l0a", "l0b"])
    dma("s", "ld_wt", T.wtb[:, 0:1], T.wt[:], [], ["wtb"])
    dma("y", "ld_x", T.xt[:, 0:4096], T.x[:], [], ["x"], 8000)
    dma("s", "ld_ch", T.rec0[:, 0:256], T.ch[:], [], ["c0a", "c0b"])
    dma("s", "ld_fl", T.ff[:], T.fl[:], [], ["ffa", "ffb"])
    ms(M("ON"), 1.0, ["ON"]); ms(T.onef[:], 1.0, ["onef"]); ms(T.wl[:], 0.0, ["wl0"], 1032)
    for nm in ("h1a", "h1b", "h2a", "h2b"):
        fill(nm, 2048, 1, nm)
    fill("mk5", 5120, 1, "mk5"); fill("cl", 2064, 0, "cl0"); fill("mo", 2064, 0, "mo0")
    for nm, st in (("jio", [[1, 16]]), ("c80", [[1280, 8]]), ("c16", [[256, 16]])):
        gp("iota", [], [nm], T[nm][:], st, 0, 0, allow_small_or_imprecise_dtypes=True)
    gp("sel", ["ON"], ["I"], M("I"), M("ON"), [[-1, 128]], OP.is_equal, 0.0, 0, 1)
    gp("sel", ["ON"], ["tmpm"], T.tmpm[:], M("ON"), [[-16, 8], [0, 16]], OP.is_ge, 0.0, 0, 1)
    gp("sel", ["tmpm"], ["B1"], M("B1"), T.tmpm[:], [[16, 8], [0, 16]], OP.is_ge, 0.0, 15, -1)
    gp("sel", ["B1"], ["LT"], M("LT"), M("B1"), [[1, 128]], OP.is_gt, 0.0, 0, -1)
    gp("sel", ["B1"], ["LE"], M("LE"), M("B1"), [[1, 128]], OP.is_ge, 0.0, 0, -1)
    for d in (1, 2, 3, 4):
        gp("sel", ["B1"], ["S%d" % d], M("S%d" % d), M("B1"), [[-1, 128]], OP.is_equal, 0.0, -d, 1)
    ts(T.tmi[:], T.sti[:], 6, None, OP.arith_shift_right, None, ["sti"], ["tmi"], 256)
    ts(T.tmj[:], T.sti[:], 63, None, OP.bitwise_and, None, ["sti"], ["tmj"], 256)
    tc(T.rec0[:, 512:768], T.tmi[:], ["tmi"], ["+s0"], 256)
    tc(T.rec0[:, 768:1024], T.tmj[:], ["tmj"], ["+s0"], 256)
    tt(T.junk[:, 0:64], T.mats[:, 0:64], T.mats[:, 64:128], OP.add, ["I"], ["f64"])
    tt(T.junk[:, 64:96], T.junk[:, 0:32], T.junk[:, 32:64], OP.add, ["f64"], ["f32"])
    tt(T.e16[:], T.junk[:, 64:80], T.junk[:, 80:96], OP.add, ["f32"], ["e16"])
    tt(T.jt[:], T.e16[:], T.jio[:], OP.mult, ["e16", "jio"], ["jt"])
    co = lambda j: T.co[:, j:j + 1]
    vop("tr", 120, ["jt"], ["co0"], co(0), T.jt[:], AxisListType.X, OP.add)
    for k in (1, 2, 3):
        ts(co(k), co(0), float(-k), None, OP.add, None, ["co0"], ["co%d" % k])
        ts(co(4 + k), co(0), -1.0, float(k), OP.mult, OP.add, ["co0"], ["co%d" % (4 + k)])
    ts(co(4), co(0), 28.0, None, OP.add, None, ["co0"], ["co4"])
    ts(co(8), co(0), 5.0, 4.0, OP.mult, OP.add, ["co0"], ["co8"])
    ts(co(9), T.wtb[:, 0:1], 64.0, None, OP.mult, None, ["wtb"], ["co9"])
    ts(co(10), co(0), 80.0, None, OP.mult, None, ["co0"], ["co10"])
    ts(co(11), co(0), 16.0, None, OP.mult, None, ["co0"], ["co11"])
    ts(co(12), T.e16[:, 0:1], 1.0, None, OP.mult, None, ["e16"], ["co12"])
    ts(co(14), T.e16[:, 4:5], 0.03125, None, OP.mult, None, ["e16"], ["co14"])
    ts(co(13), T.e16[:, 0:1], -1.0, 1.0, OP.mult, OP.add, ["e16"], ["co13"])
    ts(T.c80[:], T.c80[:], co(10), None, OP.add, None, ["co10", "c80"], ["c80"])
    ts(T.c16[:], T.c16[:], co(11), None, OP.add, None, ["co11", "c16"], ["c16"])
    b8 = SLOT["B1"] * 128
    tc(T.b8f[:], T.mats[:, b8:b8 + 113:16], ["B1"], ["b8f"])
    for gi in range(8):
        colb = T.b8f[:, gi:gi + 1]
        sl = slice(16 * gi, 16 * gi + 129 * 15 + 1, 129)
        ts(T.wl[:, sl], T.onef[:], co(9), colb, OP.mult, OP.mult, ["onef", "co9", "b8f", "wl0"], ["+wl"])
        ts(T.cl[:, sl], T.onef[:], colb, None, OP.mult, None, ["onef", "b8f", "cl0"], ["+cl"])
        ts(T.mo[:, sl], T.onef[:], co(8), colb, OP.mult, OP.mult, ["onef", "co8", "b8f", "mo0"], ["+mo"])
    tt(T.jt[:, 1:15], T.e16[:, 1:15], T.e16[:, 2:16], OP.subtract, ["e16", "co0"], ["+jd"])
    tc(T.jt[:, 15:16], T.e16[:, 15:16], ["e16", "co0"], ["+jd"])
    tc(T.jt[:, 0:1], T.e16[:, 0:1], ["e16", "co0"], ["+jd"])
    ts(T.sd[:], T.jt[:], 0.03125, None, OP.mult, None, ["jd"], ["sd"])

    def mat(dst, src, f, r2=()):
        add([("v", cv(64, 1), lambda: g.vector.tensor_scalar(M(dst), M(src), f, None, OP.mult)),
             ("s", cs(128), lambda: g.scalar.activation(M(dst), M(src), AF.Copy, scale=f))], [src] + list(r2), [dst])

    for nm, f in (("I512", 512.0), ("I101", 101.0), ("I64", 64.0), ("I32", 32.0), ("mI", -1.0), ("I16", 16.0), ("mI4", -4.0)):
        mat(nm, "I", f)
    mat("T0", "B1", T.sd[:, 0:1], ["sd"])
    for e in range(4):
        nm = "T%d" % e
        if e:
            ms(M(nm), 0.0, [nm])
        o = SLOT[nm] * 128
        ts(T.mats[:, o:o + 113:16], T.mats[:, b8:b8 + 113:16], T.sd[:, e + 1:e + 2] if e < 3 else co(14), None, OP.mult, None, ["B1", "sd", "co14"], [nm])
    mat("DG0", "I", co(13), ["co13"]); mat("DG3", "I", co(12), ["co12"])
    for nm, v in (("kd", -215.0 / 64), ("k107", 107.5), ("km1", -1.0), ("kmh", -0.5)):
        ms(T[nm][:], v, [nm])
    for e in range(15):
        mat("L%d" % e, "B1", T.sd[:, e + 1:e + 2], ["sd"])
    for nm, f in (("mB1", -1.0), ("mB8", -8.0), ("BD32", 0.03125), ("B512", 512.0), ("BX32", 32.0)):
        mat(nm, "B1", f)
    mat("BW", "B1", co(9), ["co9"])
    for d in range(4):
        s0 = "S%d" % d if d else "I"
        tt(M("E%d" % d), M(s0), M("S%d" % (d + 1)), OP.subtract, [s0, "S%d" % (d + 1)], ["E%d" % d], 256)
    ms(M("BQ0"), 0.0, ["BQ0"])
    o = SLOT["BQ0"] * 128
    tc(T.mats[:, o:o + 113:16], T.mats[:, b8:b8 + 113:16], ["B1"], ["BQ0"])
    ms(T.mk5[:, 0:5120:5], 0.0, ["mk5"], 1024)
    ms(T.ac[:, 0:1], 0.0, ["ac0"])
    for h in "ab":
        ms(T["msk" + h][:], 0.0, ["mskz" + h], 128); ms(T["h0" + h][:], 0.0, ["h0z" + h], 256); ms(T["hn" + h][:], 0.0, ["hnz" + h], 320)
        for k in (1, 2, 3):
            for e in range(k):
                ms(T["h%d%s" % (k, h)][:, e:2048:16], 0.0, ["h%d%s" % (k, h)])

    sends = []

    def send(msg, ap, tags):
        def f():
            sends.append(("b_%s%d" % msg, put(msg, ap, via(msg, core, nxt, topo) or nxt)))
        add([("g", 1500, f)], tags, ["sent%s%d" % msg], ("send",))
        tag = {"st": "s%d", "ca": "c%da", "cb": "c%db", "la": "l%da", "lb": "l%db"}[msg[0]] % msg[1]
        add([("n", 3500, None)], ["sent%s%d" % msg], [tag], ("arr", "a_%s%d" % msg, nbits(topo.mask(via(msg, prv, core, topo) or prv, core))))

    send(("st", 1), T.rec0[:, 512:1024], ["s0"])

    def places(t, h):
        R, b, pm = T["rec%d" % t], 128 * (h == "b"), T["pm" + h]
        L = R[:, 256 + b:384 + b]
        MM(["I512", "I101", "I64", "I", "l%d" % t + h, "s%d" % t], ["#pm" + h],
           grp(pm[:, 384:512], [(M("I512"), L), (M("I101"), L), (M("I64"), R[:, 512 + b:640 + b]), (M("I"), R[:, 768 + b:896 + b])]), 128)
        ts(T["s32" + h][:], pm[:, 384:512], T.ac[:, 4 * t:4 * t + 1], None, OP.add, None, ["#pm" + h, "ac%d" % t], ["s32" + h], 128)
        ts(T["r32" + h][:], T["s32" + h][:], 4095, None, OP.bitwise_and, None, ["s32" + h], ["r32" + h], 128)
        tc(T["offs" + h][:], T["r32" + h][:], ["r32" + h], ["off" + h])

    def gather(k, h):
        w = 64 if k == 4 else 128
        for s in range(128 // w):
            c0 = 128 * (h == "b") + w * s
            act(T.zz[:, 80 * c0 + k:80 * (c0 + w) - 4 + k:5], T.xt[:, 0:4096].indirect(T["offs" + h][:, w * s:w * s + w]), AF.Copy,
                ["x", "off" + h], ["z%d%s%d" % (k, h, s)], 16 * w, 1.5)

    def stream(t, h):
        b = 128 * (h == "b")
        R = T["rec%d" % t]
        C, L = R[:, b:b + 128], R[:, 256 + b:384 + b]
        cg, lg = "c%d" % t + h, "l%d" % t + h
        X = lambda nm: T[nm + h]
        pu, pm, pd = X("pu"), X("pm"), X("pd")
        PU, PM, D0, D1 = "#pu" + h, "#pm" + h, "#pd0" + h, "#pd1" + h
        g_ = lambda *n: [x + h for x in n]
        win, wx = X("win"), X("wx")

        for e in range(4):
            MM(["T%d" % e, "DG0", "DG3", "kd", cg], [D0],
               grp(pd[:, e:509 + e:4], [(M("T%d" % e), C)] + ([(M("DG%d" % e), T.kd[:])] if e in (0, 3) else [])), 128)
        flex(X("t0")[:], pd[:, 0:512], AF.Copy, [D0], g_("t0"), 512, None)
        ppv = X("pp")[:, 1:256:2]
        pts = [X("pt")[:, 256 * j + 1:256 * j + 256:2] for j in range(3)] + [X("pt")[:, 768:896]]
        for j in range(3):
            cpy(X("pt")[:, 256 * j:256 * j + 255:2], L, [lg], ["lp%d%s" % (j + 1, h)])
        ts(ppv, L, -1.0, co(12), OP.add, OP.mult, [lg, "co12"], g_("pp"))
        for e in (1, 2, 3):
            ts(X("h0")[:, e:512:4], ppv, float(e), None, OP.is_lt, None, g_("pp", "h0z"), ["+h0" + h])
        scan(X("sc")[:, 0:512], X("h0")[:], X("t0")[:], OP.add, g_("h0", "t0"), g_("sc"), 512)

        def c512(y, ys):
            o, i = X("c5")[:], X("sc")[:, y:y + 127 * ys + 1:ys]
            add([("s", cs(128), lambda: g.scalar.activation(o, i, AF.Identity, scale=16384.0, bias=55040.0)),
                 ("v", cv(64, 1), lambda: g.vector.tensor_scalar(o, i, 16384.0, 55040.0, OP.mult, OP.add))], g_("sc"), g_("c5"))
            return i

        mv = c512(3, 4)
        for n in (0, 1):
            it = []
            for hb in (0, 1):
                r0 = b + 64 * n + 32 * hb
                for e in range(16):
                    it += grp(pd[:, 512 * hb + e:512 * hb + e + 497:16], [(M("L%d" % e), R[:, r0:r0 + 32]) if e < 15 else (M("I"), T.kd[:, 0:32])])
            MM(["L%d" % e for e in range(15)] + ["I", "kd", cg], [D0, D1], it, 32)
            for hb in (0, 1):
                c0 = 1024 * n + 512 * hb
                flex(X("dt")[:, c0:c0 + 512], pd[:, 512 * hb:512 * hb + 512], AF.Copy, [D1 if hb else D0], ["dt%d%s" % (2 * n + hb, h)], 512, None)
        MM(["E0", "E1", "E2", "E3", "S4", cg], [D0, D1], [x for d in range(5) for x in grp(pd[:, 128 * d:128 * d + 128], [(M("E%d" % d if d < 4 else "S4"), C)])], 128)
        for d in range(5):
            flex(X("rd")[:, d:640:5], pd[:, 128 * d:128 * d + 128], AF.Copy, [D1 if d == 4 else D0], ["rd%d%s" % (d, h)], 128, None)
        act(X("w3")[:], L, AF.Sigmoid, [lg], g_("w3"), scale=3.4657359027997265, bias=-41.58883083359672)

        zb = 80 * b
        for k in range(4):
            kk = k + 1
            gather(k, h)
            U, U2 = pu[:, 0:128], pd[:, 0:128]
            zt = ["wl", "z%d%s0" % (k, h)]
            us = [(WM("wl", m), T.zz[:, zb + 5 * m + k:zb + 5 * m + k + 80 * 127 + 1:80]) for m in range(16)]
            MM(zt, [PU], grp(U, us), 128)
            tt(X("x32")[:], U, mv, OP.mult, [PU] + g_("sc"), g_("x32"))
            tt(X("n32")[:], U, X("c5")[:], OP.add, [PU] + g_("c5"), g_("n32"))
            MM(["I32", "I", "k107"] + zt + g_("sc"), [D0], grp(U2, [(M("I32"), mv), (M("I"), T.k107[:])] + us), 128)
            ts(X("s32")[:], X("x32")[:], 3, 4095, OP.arith_shift_right, OP.bitwise_and, g_("x32"), g_("s32"), 128)
            tt(X("r32")[:], X("s32")[:], U2, OP.add, [D0] + g_("s32"), g_("r32"))
            ts(X("s32")[:], X("r32")[:], 4095, None, OP.bitwise_and, None, g_("r32"), g_("s32"), 128)
            tc(X("offs")[:], X("s32")[:], g_("s32"), ["off" + h])
            P = pts[k]
            tp = "p%d%s" % (kk, h)
            ts(X("nn")[:], X("n32")[:], 9, 3, OP.arith_shift_right, OP.bitwise_and, g_("n32"), g_("nn"), 128)
            if k == 0:
                tc(P, X("nn")[:], g_("nn"), [tp])
            else:
                tt(P, X("nn")[:], pm[:, 128:256], OP.add, [PM] + g_("nn"), [tp])
            if k < 3:
                MM(["I", tp], [PM], grp(pm[:, 128:256], [(M("I"), P)]), 128)
                ts(X("msk")[:, 1:256:2], P, co(kk), None, OP.is_ge, None, [tp, "co%d" % kk] + g_("mskz"), g_("msk"))
                scan(X("pp")[:], X("msk")[:], X("pt")[:, 256 * k:256 * kk], OP.add, [tp, "lp%d%s" % (kk, h)] + g_("msk", "mskz"), g_("pp"), 256)
                hn = "h%d" % kk
                hts = []
                for q in range(kk + 1, {1: 9, 2: 13, 3: 17}[kk]):
                    hts.append("%s%s_%d" % (hn, h, q))

                    def mk(o, i, d):
                        return [("v", cv(64, 1), lambda: g.vector.tensor_scalar(o, i, float(d), None, OP.is_lt)),
                                ("s", cs(128), lambda: g.scalar.activation(o, i, AF.Sigmoid, scale=-200.0, bias=200.0 * d - 100.0))]
                    add(mk(X(hn)[:, q - 1:2048:16], ppv, q - kk), g_("pp", hn), [hts[-1]])
                scan(X("sc")[:], X(hn)[:], X("dt")[:], OP.add, hts + g_(hn) + ["dt%d%s" % (n, h) for n in range(4)], g_("sc"), 2048)
                mv = c512(15, 16)
        gather(4, h)
        yield
        for s in (0, 1):
            o = zb + 5120 * s
            scan(T.vs[:, o:o + 5120], T.mk5[:], T.zz[:, o:o + 5120], OP.max, ["mk5", "z4%s%d" % (h, s)] + ["z%d%s0" % (k, h) for k in range(4)], ["vs%d%s" % (s, h)], 5120)
            it = []
            for m in range(16):
                it += grp(pd[:, 64 * m:64 * m + 64], [(M("I"), T.vs[:, o + 5 * m + 4:o + 5 * m + 4 + 80 * 63 + 1:80]), (M("mI"), T.ff[:, b + 64 * s:b + 64 * s + 64])])
            MM(["I", "mI", "vs%d%s" % (s, h), "ff" + h], [D0, D1], it, 64)
            act(X("gg")[:], pd[:], AF.Sign, [D0, D1], g_("gg"), 1024, bias=0.5)
            MM(["cl"] + g_("gg"), [PM], grp(pm[:, 64 * s:64 * s + 64], [(WM("cl", m), X("gg")[:, 64 * m:64 * m + 64]) for m in range(16)]), 64)
        cpy(T.vs[:, zb:zb + 10240:80], T.ff[:, b:b + 128], ["ff" + h, "vs0" + h, "vs1" + h], ["vs0" + h, "vs1" + h])
        flex(X("fl")[:], pm[:, 0:128], AF.Sigmoid, [PM], g_("fl"), 128, (1.0, None, OP.is_ge), scale=200.0, bias=-100.0)
        tt(X("fw")[:], X("fl")[:], X("w3")[:], OP.mult, g_("fl", "w3"), g_("fw"), 256)
        MM(["BD32"] + g_("fw"), [PU], grp(pu[:, 0:128], [(M("BD32"), X("fw")[:])]), 128)
        tt(X("cand")[:], X("fw")[:], pu[:, 0:128], OP.is_gt, [PU] + g_("fw"), g_("cand"))
        MM(["LT"] + g_("cand"), [PU], grp(pu[:, 128:256], [(M("LT"), X("cand")[:])]), 128)
        tt(win[:], X("cand")[:], pu[:, 128:256], OP.is_gt, [PU] + g_("cand"), g_("win"))
        if h == "b" and t < 2:
            MM(["ON", "wina", "winb"], [PM], grp(pm[:, 384:512], [(M("ON"), T.wina[:]), (M("ON"), T.winb[:])]), 128)
            act(T.junk[:], pm[:, 384:512], AF.Copy, [PM], ["f64", "f32", "ac%d" % (t + 1)], accum_out=T.ac[:, 4 * t + 4:4 * t + 5])
        MM(["mo"] + g_("win"), [PU], grp(pu[:, 0:8], [(WM("mo", a), win[:, a:128:16]) for a in range(16)]), 8)
        tt(X("o32")[:], pu[:, 0:8], T.c80[:], OP.add, [PU, "c80"], g_("o32"))
        ts(X("nk")[:], pu[:, 0:8], 1.0, 4096.0, OP.is_lt, OP.mult, [PU], g_("nk"))
        tc(X("ofs")[:], X("o32")[:], g_("o32"), g_("ofs"), 64)
        tc(X("vsel")[:], T.vs[:, zb:zb + 10240].indirect(X("ofs")[:]), ["vs0" + h, "vs1" + h] + g_("ofs"), g_("vsel"), 192)
        MM(["wl"] + g_("vsel"), [PU], grp(pu[:, 8:16], [(WM("wl", a), X("vsel")[:, a:128:16]) for a in range(16)]), 8)
        tt(X("nk")[:], X("nk")[:], T.c16[:, b // 16:b // 16 + 8], OP.add, ["c16"] + g_("nk"), g_("nk"))
        tc(X("q32")[:], pu[:, 8:16], [PU], g_("q32"), 64)
        ts(X("o32")[:], X("q32")[:], 6, 15, OP.arith_shift_right, OP.bitwise_and, g_("q32"), g_("o32"))
        tt(X("q32")[:], X("o32")[:], X("nk")[:], OP.add, g_("o32", "nk"), g_("q32"))
        tc(X("of2")[:], X("q32")[:], g_("q32"), g_("of2"), 64)
        tc(T.xt[:].indirect(X("of2")[:]), X("vsel")[:], g_("of2", "vsel"), ["x"], 512)
        MM(["I", "I16", lg, "p1" + h, "p2" + h, "p3" + h, "p4" + h] + g_("win"), [D0, D1],
           [x for j in range(5) for x in grp(pd[:, 128 * j:128 * j + 128], [(M("I"), pts[j - 1] if j else L), (M("I16"), win[:])])], 128)
        flex(wx[:], pd[:, 0:640], AF.Relu, [D0, D1], g_("wx"), 640, (-16.0, 0.0, OP.add, OP.max), bias=-16.0)
        MM(["LE"] + g_("wx"), [PU], grp(pu[:, 128:256], [(M("LE"), wx[:, 0:128])]), 128)
        for d in (1, 2, 3, 4):
            flex(X("hn")[:, d:640:5], pu[:, 128:256], AF.Sigmoid, [PU, "hnz" + h], ["+hn" + h], 128, (float(d), None, OP.is_lt), scale=-200.0, bias=200.0 * d - 100.0)
        scan(X("scn")[:], X("hn")[:], X("rd")[:], OP.add, g_("hn") + ["rd%d%s" % (d, h) for d in range(5)], g_("scn"), 640)
        NRt = T["nr%d" % t]
        flex(NRt[:, b:b + 128], X("scn")[:, 4:640:5], AF.Copy, g_("scn"), ["nc%d%s" % (t, h)], 64, None)
        if t < 2:
            send(("c" + h, t + 1), NRt[:, b:b + 128], ["nc%d%s" % (t, h)])
        MM(["B1", "BX32"] + g_("wx", "win"), [D0], [x for j in (1, 2, 3, 4) for x in grp(pd[:, 128 * j - 128:128 * j],
           [(M("B1"), wx[:, 128 * j:128 * j + 128])] + ([(M("BX32"), win[:])] if j == 4 else []))], 128)
        ts(X("m4")[:], pd[:, 384:512], co(4), None, OP.is_equal, None, [D0, "co4"], g_("m4"), 128)
        for j in (1, 2, 3):
            act(X("ax")[:, 128 * j - 128:128 * j], pd[:, 128 * j - 128:128 * j], AF.Abs, [D0, "co%d" % (4 + j)], ["+ax" + h], bias=co(4 + j))
        tc(X("z4")[:], T.zz[:, zb:zb + 10240].indirect(X("ofs")[:]), g_("ofs") + ["z4%s1" % h] + ["z%d%s0" % (k, h) for k in range(5)], g_("z4"), 192)
        tt(X("t4")[:], X("m4")[:], X("scn")[:, 4:640:5], OP.mult, g_("m4", "scn"), g_("t4"), 256)
        MM(["BW", "B512"] + g_("z4", "t4"), [PU], grp(pu[:, 0:128], [(M("BW"), X("z4")[:]), (M("B512"), X("t4")[:])]), 128)
        tc(X("n4")[:], pu[:, 0:128], [PU], g_("n4"))
        ts(X("n5")[:], X("n4")[:], 9, 3, OP.arith_shift_right, OP.bitwise_and, g_("n4"), g_("n5"), 128)
        tt(X("n4m")[:], X("n5")[:], X("m4")[:], OP.mult, g_("n5", "m4"), g_("n4m"), 256)
        it = []
        for j in (1, 2, 3):
            it += grp(pd[:, 384 + 128 * j:512 + 128 * j], [(M("B1"), wx[:, 128 * j + 128:128 * j + 256]), (M("mB1"), wx[:, 128 * j:128 * j + 128]), (M("mI4"), X("ax")[:, 128 * j - 128:128 * j])])
        it += grp(pd[:, 896:1024], [(M("I"), L), (M("mB8"), win[:]), (M("I"), T.km1[:])])
        MM(["B1", "mB1", "mI4", "mB8", "I", "km1", lg] + g_("wx", "ax", "win"), [D1], it, 128)
        flex(X("ex")[:], pd[:, 512:1024], AF.Relu, [D1], g_("ex"), 512, (0.0, None, OP.max))
        MM(["BQ0", "I"] + g_("wx", "ex", "n4m"), [PU],
           grp(pu[:, 256:384], [(M("BQ0"), wx[:, 128:256])] + [(M("I"), X("ex")[:, 128 * j:128 * j + 128]) for j in range(4)] + [(M("I"), X("n4m")[:])]), 128)
        flex(NRt[:, 256 + b:384 + b], pu[:, 256:384], AF.Identity, [PU], ["nl%d%s" % (t, h)], 128, (1.0, None, OP.add), bias=1.0)
        if t < 2:
            send(("l" + h, t + 1), NRt[:, 256 + b:384 + b], ["nl%d%s" % (t, h)])
        MM(["I", "kmh", "ff" + h] + g_("vsel"), [PM], grp(pm[:, 384:512], [(M("I"), T.ff[:, b:b + 128]), (M("I"), X("vsel")[:]), (M("I"), T.kmh[:])]), 128)
        act(X("f1")[:], pm[:, 384:512], AF.Identity, [PM], g_("f1"), scale=0.5, bias=12582912.0)
        act(T.ff[:, b:b + 128], X("f1")[:], AF.Identity, g_("f1"), ["ff" + h], bias=-12582912.0)

    for t in range(3):
        for h in "ab":
            places(t, h)
        if t == 1:
            send(("st", 2), T.rec1[:, 512:1024], ["s1"])
        for part in [stream(t, h) for h in "ab"] * 2:
            next(part, None)
    for hb in (0, 1):
        MM(["I", "x"], ["#pu" + "ab"[hb]], grp(T["pu" + "ab"[hb]][:, 0:128], [(M("I"), T.xt[:, 2048 * hb + a:2048 * hb + 2048:16]) for a in range(16)]), 128)
        act(T.ysb[:, 128 * hb:128 * hb + 128], T["pu" + "ab"[hb]][:, 0:128], AF.Copy, ["#pu" + "ab"[hb]], ["ysb%d" % hb])
    dma("y", "o_c", T.yc[:], T.nr2[:, 0:256], ["nc2a", "nc2b"], [])
    dma("y", "o_l", T.yl[:], T.nr2[:, 256:512], ["nl2a", "nl2b"], [])
    dma("y", "o_f", T.yf[:], T.ff[:], ["ffa", "ffb"], [])
    dma("y", "o_s", T.ys[:], T.ysb[:], ["ysb0", "ysb1"], [])

    Q = {"v": g.vector, "s": g.scalar, "t": g.tensor, "g": g, "y": g.sync}
    cnt = {"v": 0, "s": 0, "t": 0, "g": 0}
    known = {q: {} for q in Q}
    lw, rd, bank = {}, {}, {}
    if not KEEP:
        KEEP.append(order([(n[0], n[1], n[2], n[3][0]) for n in nodes]))
    for _, j, a in KEEP[0]:
        (q, _, f), (_, r, w, kind) = nodes[j][0][a], nodes[j]
        if kind[0] == "arr":
            for t in w:
                lw[t], rd[t] = [(kind[1], kind[2], {})], []
            continue
        own, evs = "e_" + q, []
        for t in r + w:
            if t[0] == "#":
                evs += [e for e in bank.get(t, {}).values() if e[0] != own]
            elif t[0] == "+":
                evs += rd.get(t[1:], [])
            else:
                evs += lw.get(t, []) + (rd.get(t, []) if t in w else [])
        best = {}
        for sem, val, clk in evs:
            if known[q].get(sem, 0) < val and (sem not in best or best[sem][0] < val):
                best[sem] = (val, clk)
        for sem, (val, clk) in best.items():
            if not any(o != sem and best[o][1].get(sem, 0) >= val for o in best):
                Q[q].wait_ge(T.sem[sem], val)
        for sem, (val, clk) in best.items():
            for k, x in list(clk.items()) + [(sem, val)]:
                known[q][k] = max(known[q].get(k, 0), x)
        if kind[0] == "send":
            f()
            ev = (sends[-1][0], sends[-1][1], dict(known[q]))
        elif kind[0] == "dma":
            f().then_inc(T.sem[kind[1]], 16)
            ev = (kind[1], 16, dict(known[q]))
        else:
            cnt[q] += 1
            f().then_inc(T.sem[own], 1)
            ev = (own, cnt[q], dict(known[q]))
            ev[2][own] = cnt[q]
        for t in set(r + w):
            if t[0] == "#":
                bank.setdefault(t, {})[ev[0]] = ev
            elif t[0] == "+":
                lw.setdefault(t[1:], []).append(ev)
            elif t in w:
                lw[t], rd[t] = [ev], []
            else:
                rd[t] = [e for e in rd.get(t, []) if e[0] != ev[0]] + [ev]
    for q in ("v", "s", "t", "g"):
        g.wait_ge(T.sem["e_" + q], cnt[q])
    for s in ("o_c", "o_l", "o_f", "o_s"):
        g.wait_ge(T.sem[s], 16)
    for s, n in sends:
        g.wait_ge(T.sem[s], n)
